import numpy as np
import ml_dtypes


def mxq(x, axis, fmt="e4m3"):
    dtype, down = {"e4m3": (ml_dtypes.float8_e4m3fn, 7), "e5m2": (ml_dtypes.float8_e5m2, 14)}[fmt]
    v = np.moveaxis(np.asarray(x, np.float32).astype(ml_dtypes.bfloat16).astype(np.float64), axis, -1)
    blocks = v.reshape(v.shape[:-1] + (-1, 32))
    amax = np.abs(blocks).max(-1, keepdims=True)
    byte = np.maximum(np.where(amax > 0, np.frexp(amax)[1] - 1 + 127, 0) - down, 1)
    scale = np.exp2(byte - 127.0)
    codes = (blocks / scale).astype(np.float32).astype(dtype).astype(np.float64)
    return np.moveaxis((codes * scale).reshape(v.shape), -1, axis)


WIDE = False


def mx_kscale(k):
    if not WIDE:
        return np.ones(k)
    levels = np.array([10, -10, 5, -5, 0])
    if k % 512:
        return np.exp2(np.random.permutation(np.resize(levels, k // 32))).repeat(32)
    a = np.empty((k // 512, 16))
    for p in range(k // 512):
        a[p, :8] = np.random.permutation(np.resize(levels, 8))
        for g in range(8):
            far = levels[np.abs(levels - a[p, g]) >= 10]
            a[p, g + 8] = far[np.random.randint(len(far))]
    return np.exp2(a.ravel()).repeat(32)


def f64(x):
    return np.asarray(x).astype(np.float64)


def striped8(idx):
    return np.concatenate([x.reshape(-1, 16).T for x in idx]).astype(np.uint16)


def runs(offs, k):
    lists = np.stack([offs[16 * r : 16 * r + 16].T.reshape(-1) for r in range(8)]).astype(np.int64)
    return lists[np.arange(k) % 512 // 64]


def pack_weight(w):
    k, n = w.shape
    w = f64(np.asarray(w, np.float32).astype(ml_dtypes.bfloat16)).reshape(k // 32, 32, n)
    amax = np.abs(w).max(1)
    byte = np.clip(np.where(amax > 0, np.frexp(amax)[1] - 1 + 127 - 7, 1), 1, 254)
    scaled = (w * np.exp2(127.0 - byte)[:, None, :]).reshape(k, n).astype(np.float32)
    words = np.ascontiguousarray(scaled.reshape(k // 512, 128, 4, n).transpose(0, 1, 3, 2)).astype(ml_dtypes.float8_e4m3fn).view(np.uint8)
    return words, np.ascontiguousarray(byte.astype(np.uint8).reshape(k // 512, 16, n))


def unpack_weight(words, scales):
    g, p, n, _ = words.shape
    vals = np.ascontiguousarray(words).view(ml_dtypes.float8_e4m3fn).astype(np.float64) * np.repeat(np.exp2(scales.astype(np.float64) - 127.0), 8, axis=1)[..., None]
    return vals.transpose(0, 1, 3, 2).reshape(g * 512, n)


E2M1 = np.array([0.0, 0.5, 1.0, 1.5, 2.0, 3.0, 4.0, 6.0, -0.0, -0.5, -1.0, -1.5, -2.0, -3.0, -4.0, -6.0])


def pack_fp4(w):
    k, n = w.shape
    w = f64(np.asarray(w, np.float32).astype(ml_dtypes.bfloat16)).reshape(k // 32, 32, n)
    amax = np.abs(w).max(1)
    mant, ex = np.frexp(amax / 6.0)
    byte = np.clip(np.where(amax > 0, np.where(mant > 0.5, ex, ex - 1) + 127, 1), 1, 254)
    scaled = (w * np.exp2(127.0 - byte)[:, None, :]).reshape(k, n).astype(np.float32)
    c = np.ascontiguousarray(scaled.reshape(k // 512, 128, 4, n).transpose(0, 1, 3, 2)).astype(ml_dtypes.float4_e2m1fn).view(np.uint8) & 0xF
    words = (c[..., 0::2] | (c[..., 1::2] << 4)).reshape(k // 512, 128, 2 * n)
    return np.ascontiguousarray(words), np.ascontiguousarray(byte.astype(np.uint8).reshape(k // 512, 16, n))


def unpack_fp4(words, scales):
    g, _, n = scales.shape
    words = np.ascontiguousarray(words).reshape(g, 128, n, 2)
    nib = np.empty((g, 128, n, 4), np.uint8)
    nib[..., 0::2] = words & 0xF
    nib[..., 1::2] = words >> 4
    vals = E2M1[nib] * np.repeat(np.exp2(scales.astype(np.float64) - 127.0), 8, axis=1)[..., None]
    return vals.transpose(0, 1, 3, 2).reshape(g * 512, n)


def gelu(v):
    return 0.5 * v * (1.0 + np.tanh(np.sqrt(2.0 / np.pi) * (v + 0.044715 * v**3)))

def planes(y):
    n, m = y.shape
    v = y.astype(np.float32).astype(ml_dtypes.bfloat16).astype(np.float64).reshape(n // 32, 32, m)
    top = np.abs(v).max(1)
    byte = np.clip(np.where(top > 0, np.frexp(top)[1] - 1 + 127 - 7, 1), 1, 254)
    codes = (v * np.exp2(127.0 - byte)[:, None, :]).reshape(n, m).astype(np.float32).astype(ml_dtypes.float8_e4m3fn).view(np.uint8)
    words = codes.reshape(n // 512, 128, 4, m).transpose(0, 1, 3, 2)
    return np.ascontiguousarray(words), np.ascontiguousarray(byte.astype(np.uint8).reshape(n // 512, 16, m))


K, T, S, N, H = 512, 2048, 512, 512, 512


def setup_inputs():
    n = np.random.standard_normal
    s = mx_kscale(K)[:, None]
    u = mx_kscale(H)
    packed_xT = pack_weight(n((K, T)) * s)
    packed_w2 = pack_fp4(n((H, N)) / np.sqrt(H) / u[:, None])
    return {
        "x_words": packed_xT[0],
        "x_scales": packed_xT[1],
        "w1": (n((K, H)) / np.sqrt(K) / s * u).astype(np.float32),
        "w2_words": packed_w2[0],
        "w2_scales": packed_w2[1],
        "offs": striped8(np.stack([np.random.permutation(T)[:S] for _ in range(8)])),
        "back": striped8(np.stack([np.random.permutation(S) for _ in range(8)])),
    }


def reference(x_words, x_scales, w1, w2_words, w2_scales, offs, back):
    xq = unpack_weight(x_words, x_scales)[np.arange(K)[:, None], runs(offs, K)]
    y = mxq(f64(w1), 0, "e4m3").T @ xq
    z = gelu(y[np.arange(H)[:, None], runs(back, H)])
    out_0 = unpack_fp4(w2_words, w2_scales).T @ mxq(z, 0, "e4m3")
    return (out_0,) + planes(out_0)

@@ -1,0 +1,172 @@
+from contextlib import ExitStack
+
+import concourse.mybir as mybir
+
+K, T, S, H, N = 512, 2048, 512, 512, 512
+FLOPS = 2 * K * H * S + 2 * H * N * S
+
+F32 = mybir.dt.float32
+BF16 = mybir.dt.bfloat16
+I32 = mybir.dt.int32
+U32 = mybir.dt.uint32
+U16 = mybir.dt.uint16
+U8 = mybir.dt.uint8
+FP8X4 = mybir.dt.float8_e4m3fn_x4
+FP4X4 = mybir.dt.float4_e2m1fn_x4
+GELU = mybir.ActivationFunctionType.Gelu_apprx_tanh
+
+P = 128
+PACK = 4
+HALF = S // 2
+CHUNK = 128
+
+
+def tile_picked_permun_gelu_po_kernel(
+    tc, x_words, x_scales, w1, w2_words, w2_scales, offs, back, out_0, out_1, out_2
+):
+    nc = tc.nc
+    with ExitStack() as ctx:
+        keep = ctx.enter_context(tc.tile_pool(name="keep", bufs=1))
+        psum = ctx.enter_context(tc.psum_pool(name="psum", bufs=8))
+
+        offs_sb = keep.tile([P, S // 16], U16, name="offs_sb")
+        back_sb = keep.tile([P, S // 16], U16, name="back_sb")
+        xs_all = keep.tile([P, T], U8, name="xs_all", align_bytes=64)
+        xs_mm = keep.tile([P, S], U8, name="xs_mm", align_bytes=64)
+        w2s_raw = keep.tile([P, N], U8, name="w2s_raw", tag="planes01", align_bytes=64)
+        w1_raw = keep.tile([P, PACK, H], F32, name="w1_raw", align_bytes=64)
+        xw_all = keep.tile([P, T], I32, name="xw_all", tag="xw_all", align_bytes=64)
+        w2w_raw = keep.tile([P, 2 * N], U8, name="w2w_raw", align_bytes=64)
+
+        nc.vector.memset(xs_all[:].bitcast(I32), 0)
+        nc.vector.memset(xs_mm[:].bitcast(I32), 0)
+        nc.gpsimd.memset(w2s_raw[:].bitcast(I32), 0)
+
+        nc.sync.dma_start(offs_sb[:], offs)
+        nc.scalar.dma_start(xs_all[0:P:8, :].bitcast(I32), x_scales[0].bitcast(I32))
+        nc.sync.dma_start(w1_raw[:], w1.rearrange("(p j) c -> p j c", j=PACK))
+        nc.sync.dma_start(xw_all[:], x_words[0].rearrange("p n r -> p (n r)").bitcast(I32))
+        nc.sync.dma_start(w2w_raw[:].bitcast(I32), w2_words[0].bitcast(I32))
+        nc.sync.dma_start(back_sb[:], back)
+        for q in range(4):
+            nc.gpsimd.dma_start(
+                w2s_raw[32 * q : 32 * q + 4, :].bitcast(I32), w2_scales[0, 4 * q : 4 * q + 4, :].bitcast(I32)
+            )
+
+        xs_picked = keep.tile([P, S], U8, name="xs_picked", align_bytes=64)
+        nc.vector.tensor_copy(xs_picked[:], xs_all[:].indirect(offs_sb[:]))
+        for q in range(4):
+            nc.scalar.dma_start(
+                xs_mm[32 * q : 32 * q + 4, :].bitcast(I32), xs_picked[32 * q : 32 * q + 32 : 8, :].bitcast(I32)
+            )
+
+        w1_bf = keep.tile([P, PACK * H], BF16, name="w1_bf", align_bytes=64)
+        cast_out = w1_bf[:].rearrange("p (t m j) -> p m t j", t=PACK, j=PACK)
+        cast_in = w1_raw[:].rearrange("p j (m t) -> p m t j", t=PACK)
+        nc.vector.tensor_copy(cast_out, cast_in)
+        w1_codes = keep.tile([P, H], U32, name="w1_codes", align_bytes=64)
+        w1_scale = keep.tile([P, H], U8, name="w1_scale", align_bytes=64)
+        nc.vector.quantize_mx(w1_codes[:].bitcast(FP8X4), w1_scale[:], w1_bf[:])
+
+        w2s = keep.tile([P, N], U8, name="w2s", align_bytes=64)
+        nc.vector.tensor_copy(
+            w2s[:].rearrange("p (t m) -> p t m", t=PACK), w2s_raw[:].rearrange("p (m t) -> p t m", t=PACK)
+        )
+
+        xw = []
+        for h in range(2):
+            picked = keep.tile([P, HALF], U32, name="xw_picked%d" % h, align_bytes=64)
+            nc.vector.tensor_copy(picked[:], xw_all[:].bitcast(U32).indirect(offs_sb[:, 16 * h : 16 * h + 16]))
+            xw.append(picked)
+
+        w2w = keep.tile([P, 2 * N], U8, name="w2w", tag="xw_all", align_bytes=64)
+        nc.vector.tensor_copy(
+            w2w[:].rearrange("p (t m b) -> p t m b", t=PACK, b=2),
+            w2w_raw[:].rearrange("p (m t b) -> p t m b", t=PACK, b=2),
+        )
+
+        act = [keep.tile([P, S], F32, name="act%d" % t, align_bytes=64) for t in range(PACK)]
+        for t, h in [(0, 0), (1, 0), (0, 1), (1, 1), (2, 0), (2, 1), (3, 0), (3, 1)]:
+            bank = psum.tile([P, HALF], F32, name="y_bank", tag="bank")
+            cols = slice(HALF * h, HALF * (h + 1))
+            nc.tensor.matmul_mx(
+                bank[:],
+                lhsT=w1_codes[:, P * t : P * (t + 1)].bitcast(FP8X4),
+                lhsT_scale=w1_scale[:, P * t : P * (t + 1)],
+                rhs=xw[h][:].bitcast(FP8X4),
+                rhs_scale=xs_mm[:, cols],
+                start=True,
+                stop=True,
+            )
+            nc.scalar.activation(act[t][:, cols], bank[:], GELU)
+
+        out_rows = out_0.rearrange("(p t) j -> p t j", t=PACK)
+        out_words = out_1[0].rearrange("p n r -> p (n r)").bitcast(I32)
+        out_codes = keep.tile([P, S], U32, name="out_codes", align_bytes=64)
+        out_scale = keep.tile([P, S], U8, name="out_scale", align_bytes=64)
+
+        def fetch(first, width, tag):
+            planes = keep.tile([P, PACK, width], BF16, name="planes%d" % first, tag=tag, align_bytes=64)
+            for t in range(PACK):
+                nc.vector.tensor_copy(
+                    planes[:, t, :], act[t][:].indirect(back_sb[:, first // 16 : (first + width) // 16])
+                )
+            return planes
+
+        def weave(planes, first, c, engine_copy, tag):
+            woven = keep.tile([P, CHUNK, PACK], BF16, name="woven%d" % c, tag=tag, align_bytes=64)
+            engine_copy(woven[:], planes[:, :, first : first + CHUNK].rearrange("p t n -> p n t"))
+            return woven
+
+        def second_product(woven, c):
+            z_codes = keep.tile([P, CHUNK], U32, name="z_codes%d" % c, align_bytes=64)
+            z_scale = keep.tile([P, CHUNK], U8, name="z_scale%d" % c, align_bytes=64)
+            nc.vector.quantize_mx(z_codes[:].bitcast(FP8X4), z_scale[:], woven[:].rearrange("p n t -> p (n t)"))
+            bank = psum.tile([P, PACK, CHUNK], F32, name="out_bank", tag="bank")
+            for t in range(PACK):
+                nc.tensor.matmul_mx(
+                    bank[:, t, :],
+                    lhsT=w2w[:, 2 * P * t : 2 * P * (t + 1)].bitcast(FP4X4),
+                    lhsT_scale=w2s[:, P * t : P * (t + 1)],
+                    rhs=z_codes[:].bitcast(FP8X4),
+                    rhs_scale=z_scale[:],
+                    start=True,
+                    stop=True,
+                )
+            return bank
+
+        def hand_out(bank, c, round_copy, from_bank):
+            cols = slice(CHUNK * c, CHUNK * (c + 1))
+            result = keep.tile([P, PACK, CHUNK], F32, name="result%d" % c, align_bytes=64)
+            rounded = keep.tile([P, CHUNK, PACK], BF16, name="rounded%d" % c, align_bytes=64)
+            if from_bank:
+                round_copy(rounded[:], bank[:].rearrange("p t n -> p n t"))
+            nc.scalar.copy(result[:], bank[:])
+            if not from_bank:
+                round_copy(rounded[:], result[:].rearrange("p t n -> p n t"))
+            nc.sync.dma_start(out_rows[:, :, cols], result[:])
+            nc.vector.quantize_mx(
+                out_codes[:, cols].bitcast(FP8X4), out_scale[:, cols], rounded[:].rearrange("p n t -> p (n t)")
+            )
+            nc.sync.dma_start(out_words[:, cols], out_codes[:, cols].bitcast(I32))
+
+        planes01 = fetch(0, 2 * CHUNK, "planes01")
+        woven0 = weave(planes01, 0, 0, nc.scalar.copy, "woven0")
+        woven1 = weave(planes01, CHUNK, 1, nc.scalar.copy, "woven1")
+        planes2 = fetch(2 * CHUNK, CHUNK, "planes2")
+        bank0 = second_product(woven0, 0)
+        bank1 = second_product(woven1, 1)
+        woven2 = weave(planes2, 0, 2, nc.scalar.copy, "woven2")
+        planes3 = fetch(3 * CHUNK, CHUNK, "woven1")
+        bank2 = second_product(woven2, 2)
+        woven3 = weave(planes3, 0, 3, nc.vector.tensor_copy, "woven3")
+        bank3 = second_product(woven3, 3)
+        hand_out(bank0, 0, nc.scalar.copy, True)
+        hand_out(bank1, 1, nc.vector.tensor_copy, False)
+        hand_out(bank2, 2, nc.vector.tensor_copy, False)
+        hand_out(bank3, 3, nc.vector.tensor_copy, True)
+
+        out_scale_rows = out_2[0].bitcast(I32)
+        for q in range(4):
+            queue = nc.sync if q % 2 else nc.scalar
+            queue.dma_start(out_scale_rows[4 * q : 4 * q + 4, :], out_scale[32 * q : 32 * q + 4, :].bitcast(I32))

@@ -27,31 +27,35 @@ def tile_picked_permun_gelu_po_kernel(
     nc = tc.nc
     with ExitStack() as ctx:
         keep = ctx.enter_context(tc.tile_pool(name="keep", bufs=1))
+        shared = ctx.enter_context(tc.tile_pool(name="shared", bufs=1))
         psum = ctx.enter_context(tc.psum_pool(name="psum", bufs=8))
 
         offs_sb = keep.tile([P, S // 16], U16, name="offs_sb")
         back_sb = keep.tile([P, S // 16], U16, name="back_sb")
         xs_all = keep.tile([P, T], U8, name="xs_all", align_bytes=64)
         xs_mm = keep.tile([P, S], U8, name="xs_mm", align_bytes=64)
-        w2s_raw = keep.tile([P, N], U8, name="w2s_raw", tag="planes01", align_bytes=64)
         w1_raw = keep.tile([P, PACK, H], F32, name="w1_raw", align_bytes=64)
-        xw_all = keep.tile([P, T], I32, name="xw_all", tag="xw_all", align_bytes=64)
-        w2w_raw = keep.tile([P, 2 * N], U8, name="w2w_raw", align_bytes=64)
+        xw_all = shared.tile([P, T], I32, name="xw_all", align_bytes=64, offset=0)
+        w2w_raw = shared.tile([P, 2 * N], U8, name="w2w_raw", align_bytes=64, offset=4 * T)
+        w2s_raw = keep.tile([P, N], U8, name="w2s_raw", align_bytes=64)
 
         nc.vector.memset(xs_all[:].bitcast(I32), 0)
-        nc.vector.memset(xs_mm[:].bitcast(I32), 0)
         nc.gpsimd.memset(w2s_raw[:].bitcast(I32), 0)
+        nc.vector.memset(xs_mm[:].bitcast(I32), 0)
+
+        def load_w2_scale_rows(q):
+            nc.sync.dma_start(
+                w2s_raw[32 * q : 32 * q + 4, :].bitcast(I32), w2_scales[0, 4 * q : 4 * q + 4, :].bitcast(I32)
+            )
 
         nc.sync.dma_start(offs_sb[:], offs)
-        nc.scalar.dma_start(xs_all[0:P:8, :].bitcast(I32), x_scales[0].bitcast(I32))
+        nc.sync.dma_start(back_sb[:], back)
+        for q in range(4):
+            load_w2_scale_rows(q)
+        nc.sync.dma_start(xs_all[0:P:8, :].bitcast(I32), x_scales[0].bitcast(I32))
         nc.sync.dma_start(w1_raw[:], w1.rearrange("(p j) c -> p j c", j=PACK))
         nc.sync.dma_start(xw_all[:], x_words[0].rearrange("p n r -> p (n r)").bitcast(I32))
         nc.sync.dma_start(w2w_raw[:].bitcast(I32), w2_words[0].bitcast(I32))
-        nc.sync.dma_start(back_sb[:], back)
-        for q in range(4):
-            nc.gpsimd.dma_start(
-                w2s_raw[32 * q : 32 * q + 4, :].bitcast(I32), w2_scales[0, 4 * q : 4 * q + 4, :].bitcast(I32)
-            )
 
         xs_picked = keep.tile([P, S], U8, name="xs_picked", align_bytes=64)
         nc.vector.tensor_copy(xs_picked[:], xs_all[:].indirect(offs_sb[:]))
@@ -60,18 +64,25 @@ def tile_picked_permun_gelu_po_kernel(
                 xs_mm[32 * q : 32 * q + 4, :].bitcast(I32), xs_picked[32 * q : 32 * q + 32 : 8, :].bitcast(I32)
             )
 
-        w1_bf = keep.tile([P, PACK * H], BF16, name="w1_bf", align_bytes=64)
-        cast_out = w1_bf[:].rearrange("p (t m j) -> p m t j", t=PACK, j=PACK)
-        cast_in = w1_raw[:].rearrange("p j (m t) -> p m t j", t=PACK)
-        nc.vector.tensor_copy(cast_out, cast_in)
-        w1_codes = keep.tile([P, H], U32, name="w1_codes", align_bytes=64)
-        w1_scale = keep.tile([P, H], U8, name="w1_scale", align_bytes=64)
-        nc.vector.quantize_mx(w1_codes[:].bitcast(FP8X4), w1_scale[:], w1_bf[:])
-
         w2s = keep.tile([P, N], U8, name="w2s", align_bytes=64)
         nc.vector.tensor_copy(
             w2s[:].rearrange("p (t m) -> p t m", t=PACK), w2s_raw[:].rearrange("p (m t) -> p t m", t=PACK)
         )
+
+        w1_bf = keep.tile([P, PACK * H], BF16, name="w1_bf", align_bytes=64)
+        cast_out = w1_bf[:].rearrange("p (t m j) -> p m t j", t=PACK, j=PACK)
+        cast_in = w1_raw[:].rearrange("p j (m t) -> p m t j", t=PACK)
+        for pair in range(2):
+            nc.vector.tensor_copy(cast_out[:, :, 2 * pair : 2 * pair + 2], cast_in[:, :, 2 * pair : 2 * pair + 2])
+        w1_codes = keep.tile([P, H], U32, name="w1_codes", align_bytes=64)
+        w1_scale = keep.tile([P, H], U8, name="w1_scale", align_bytes=64)
+        for pair in range(2):
+            cols = slice(2 * P * pair, 2 * P * (pair + 1))
+            nc.vector.quantize_mx(
+                w1_codes[:, cols].bitcast(FP8X4),
+                w1_scale[:, cols],
+                w1_bf[:, 2 * P * PACK * pair : 2 * P * PACK * (pair + 1)],
+            )
 
         xw = []
         for h in range(2):
@@ -79,7 +90,7 @@ def tile_picked_permun_gelu_po_kernel(
             nc.vector.tensor_copy(picked[:], xw_all[:].bitcast(U32).indirect(offs_sb[:, 16 * h : 16 * h + 16]))
             xw.append(picked)
 
-        w2w = keep.tile([P, 2 * N], U8, name="w2w", tag="xw_all", align_bytes=64)
+        w2w = shared.tile([P, 2 * N], U8, name="w2w", align_bytes=64, offset=0)
         nc.vector.tensor_copy(
             w2w[:].rearrange("p (t m b) -> p t m b", t=PACK, b=2),
             w2w_raw[:].rearrange("p (m t b) -> p t m b", t=PACK, b=2),
@@ -105,27 +116,26 @@ def tile_picked_permun_gelu_po_kernel(
         out_codes = keep.tile([P, S], U32, name="out_codes", align_bytes=64)
         out_scale = keep.tile([P, S], U8, name="out_scale", align_bytes=64)
 
-        def fetch(first, width, tag):
-            planes = keep.tile([P, PACK, width], BF16, name="planes%d" % first, tag=tag, align_bytes=64)
-            for t in range(PACK):
+        def fetch(planes, ts, first, width):
+            for slot, t in enumerate(ts):
                 nc.vector.tensor_copy(
-                    planes[:, t, :], act[t][:].indirect(back_sb[:, first // 16 : (first + width) // 16])
+                    planes[:, slot, :], act[t][:].indirect(back_sb[:, first // 16 : (first + width) // 16])
                 )
-            return planes
 
-        def weave(planes, first, c, engine_copy, tag):
-            woven = keep.tile([P, CHUNK, PACK], BF16, name="woven%d" % c, tag=tag, align_bytes=64)
-            engine_copy(woven[:], planes[:, :, first : first + CHUNK].rearrange("p t n -> p n t"))
+        def weave(planes, name, engine_copy):
+            woven = keep.tile([P, planes.shape[2], PACK], BF16, name=name, tag=name, align_bytes=64)
+            engine_copy(woven[:], planes.rearrange("p t n -> p n t"))
             return woven
 
-        def second_product(woven, c):
+        def second_product(woven, c, banks):
             z_codes = keep.tile([P, CHUNK], U32, name="z_codes%d" % c, align_bytes=64)
             z_scale = keep.tile([P, CHUNK], U8, name="z_scale%d" % c, align_bytes=64)
-            nc.vector.quantize_mx(z_codes[:].bitcast(FP8X4), z_scale[:], woven[:].rearrange("p n t -> p (n t)"))
-            bank = psum.tile([P, PACK, CHUNK], F32, name="out_bank", tag="bank")
+            nc.vector.quantize_mx(z_codes[:].bitcast(FP8X4), z_scale[:], woven.rearrange("p n t -> p (n t)"))
+            per_bank = PACK // banks
+            tiles = [psum.tile([P, per_bank, CHUNK], F32, name="out_bank", tag="bank") for b in range(banks)]
             for t in range(PACK):
                 nc.tensor.matmul_mx(
-                    bank[:, t, :],
+                    tiles[t // per_bank][:, t % per_bank, :],
                     lhsT=w2w[:, 2 * P * t : 2 * P * (t + 1)].bitcast(FP4X4),
                     lhsT_scale=w2s[:, P * t : P * (t + 1)],
                     rhs=z_codes[:].bitcast(FP8X4),
@@ -133,38 +143,61 @@ def tile_picked_permun_gelu_po_kernel(
                     start=True,
                     stop=True,
                 )
-            return bank
+            return tiles
 
-        def hand_out(bank, c, round_copy, from_bank):
-            cols = slice(CHUNK * c, CHUNK * (c + 1))
-            result = keep.tile([P, PACK, CHUNK], F32, name="result%d" % c, align_bytes=64)
-            rounded = keep.tile([P, CHUNK, PACK], BF16, name="rounded%d" % c, align_bytes=64)
-            if from_bank:
-                round_copy(rounded[:], bank[:].rearrange("p t n -> p n t"))
-            nc.scalar.copy(result[:], bank[:])
-            if not from_bank:
-                round_copy(rounded[:], result[:].rearrange("p t n -> p n t"))
-            nc.sync.dma_start(out_rows[:, :, cols], result[:])
+        def columns(c):
+            return slice(CHUNK * c, CHUNK * (c + 1))
+
+        result = [keep.tile([P, PACK, CHUNK], F32, name="result%d" % c, align_bytes=64) for c in range(4)]
+        rounded = [keep.tile([P, CHUNK, PACK], BF16, name="rounded%d" % c, align_bytes=64) for c in range(4)]
+
+        def store_result(banks, c):
+            for bank, ts in banks:
+                nc.scalar.copy(result[c][:, ts, :], bank[:])
+            nc.sync.dma_start(out_rows[:, :, columns(c)], result[c][:])
+
+        def round_result(c):
+            nc.vector.tensor_copy(rounded[c][:], result[c][:].rearrange("p t n -> p n t"))
+
+        def quantize_result(c):
             nc.vector.quantize_mx(
-                out_codes[:, cols].bitcast(FP8X4), out_scale[:, cols], rounded[:].rearrange("p n t -> p (n t)")
+                out_codes[:, columns(c)].bitcast(FP8X4),
+                out_scale[:, columns(c)],
+                rounded[c][:].rearrange("p n t -> p (n t)"),
             )
-            nc.sync.dma_start(out_words[:, cols], out_codes[:, cols].bitcast(I32))
 
-        planes01 = fetch(0, 2 * CHUNK, "planes01")
-        woven0 = weave(planes01, 0, 0, nc.scalar.copy, "woven0")
-        woven1 = weave(planes01, CHUNK, 1, nc.scalar.copy, "woven1")
-        planes2 = fetch(2 * CHUNK, CHUNK, "planes2")
-        bank0 = second_product(woven0, 0)
-        bank1 = second_product(woven1, 1)
-        woven2 = weave(planes2, 0, 2, nc.scalar.copy, "woven2")
-        planes3 = fetch(3 * CHUNK, CHUNK, "woven1")
-        bank2 = second_product(woven2, 2)
-        woven3 = weave(planes3, 0, 3, nc.vector.tensor_copy, "woven3")
-        bank3 = second_product(woven3, 3)
-        hand_out(bank0, 0, nc.scalar.copy, True)
-        hand_out(bank1, 1, nc.vector.tensor_copy, False)
-        hand_out(bank2, 2, nc.vector.tensor_copy, False)
-        hand_out(bank3, 3, nc.vector.tensor_copy, True)
+        fetched = shared.tile([P, CHUNK + 2 * PACK * CHUNK], BF16, name="fetched", align_bytes=64, offset=4 * T)
+        planes01 = fetched[:, CHUNK:].rearrange("p (t n) -> p t n", t=PACK)
+        planes2 = fetched[:, : PACK * CHUNK].rearrange("p (t n) -> p t n", t=PACK)
+        planes3 = fetched[:, PACK * CHUNK : 2 * PACK * CHUNK].rearrange("p (t n) -> p t n", t=PACK)
+        fetch(planes01, range(PACK), 0, 2 * CHUNK)
+        woven01 = keep.tile([P, 2 * CHUNK, PACK], BF16, name="woven01", align_bytes=64)
+        nc.scalar.copy(woven01[:, :, 0:2], planes01[:, 0:2, :].rearrange("p t n -> p n t"))
+        for c in range(2):
+            nc.scalar.copy(woven01[:, columns(c), 2:4], planes01[:, 2:4, columns(c)].rearrange("p t n -> p n t"))
+        fetch(planes2, range(PACK), 2 * CHUNK, CHUNK)
+        (bank0,) = second_product(woven01[:, :CHUNK, :], 0, 1)
+        (bank1,) = second_product(woven01[:, CHUNK:, :], 1, 1)
+        woven2 = weave(planes2, "woven2", nc.scalar.copy)
+        fetch(planes3, range(PACK), 3 * CHUNK, CHUNK)
+        (bank2,) = second_product(woven2[:], 2, 1)
+        woven3 = weave(planes3, "woven3", nc.vector.tensor_copy)
+        low, high = second_product(woven3[:], 3, 2)
+
+        every_t = slice(0, PACK)
+        for c, bank in enumerate([bank0, bank1]):
+            store_result([(bank, every_t)], c)
+            round_result(c)
+        quantize_result(0)
+        quantize_result(1)
+        nc.sync.dma_start(out_words[:, :HALF], out_codes[:, :HALF].bitcast(I32))
+        store_result([(bank2, every_t)], 2)
+        round_result(2)
+        store_result([(low, slice(0, 2)), (high, slice(2, 4))], 3)
+        round_result(3)
+        quantize_result(2)
+        quantize_result(3)
+        nc.sync.dma_start(out_words[:, HALF:], out_codes[:, HALF:].bitcast(I32))
 
         out_scale_rows = out_2[0].bitcast(I32)
         for q in range(4):

@@ -37,37 +37,28 @@ def tile_picked_permun_gelu_po_kernel(
         w1_raw = keep.tile([P, PACK, H], F32, name="w1_raw", align_bytes=64)
         xw_all = shared.tile([P, T], I32, name="xw_all", align_bytes=64, offset=0)
         w2w_raw = shared.tile([P, 2 * N], U8, name="w2w_raw", align_bytes=64, offset=4 * T)
-        w2s_raw = keep.tile([P, N], U8, name="w2s_raw", align_bytes=64)
+        w2s_raw = shared.tile([P, N], U8, name="w2s_raw", align_bytes=64, offset=4 * T + 2 * N)
 
         nc.vector.memset(xs_all[:].bitcast(I32), 0)
         nc.gpsimd.memset(w2s_raw[:].bitcast(I32), 0)
-        nc.vector.memset(xs_mm[:].bitcast(I32), 0)
-
-        def load_w2_scale_rows(q):
-            nc.sync.dma_start(
-                w2s_raw[32 * q : 32 * q + 4, :].bitcast(I32), w2_scales[0, 4 * q : 4 * q + 4, :].bitcast(I32)
-            )
 
         nc.sync.dma_start(offs_sb[:], offs)
-        nc.sync.dma_start(back_sb[:], back)
-        for q in range(4):
-            load_w2_scale_rows(q)
-        nc.sync.dma_start(xs_all[0:P:8, :].bitcast(I32), x_scales[0].bitcast(I32))
+        for b in range(2):
+            nc.scalar.dma_start(xs_all[b:P:16, :].bitcast(I32), x_scales[0, b:16:2, :].bitcast(I32))
         nc.sync.dma_start(w1_raw[:], w1.rearrange("(p j) c -> p j c", j=PACK))
         nc.sync.dma_start(xw_all[:], x_words[0].rearrange("p n r -> p (n r)").bitcast(I32))
         nc.sync.dma_start(w2w_raw[:].bitcast(I32), w2_words[0].bitcast(I32))
+        nc.sync.dma_start(back_sb[:], back)
+        for q in range(4):
+            nc.gpsimd.dma_start(
+                w2s_raw[32 * q : 32 * q + 4, :].bitcast(I32), w2_scales[0, 4 * q : 4 * q + 4, :].bitcast(I32)
+            )
 
         xs_picked = keep.tile([P, S], U8, name="xs_picked", align_bytes=64)
         nc.vector.tensor_copy(xs_picked[:], xs_all[:].indirect(offs_sb[:]))
-        for q in range(4):
-            nc.scalar.dma_start(
-                xs_mm[32 * q : 32 * q + 4, :].bitcast(I32), xs_picked[32 * q : 32 * q + 32 : 8, :].bitcast(I32)
-            )
-
-        w2s = keep.tile([P, N], U8, name="w2s", align_bytes=64)
-        nc.vector.tensor_copy(
-            w2s[:].rearrange("p (t m) -> p t m", t=PACK), w2s_raw[:].rearrange("p (m t) -> p t m", t=PACK)
-        )
+        nc.vector.tensor_copy(xs_mm[:].bitcast(I32), xs_picked[:].bitcast(I32))
+        for b in range(2):
+            nc.scalar.dma_start(xs_mm[2 + b : P : 32, :].bitcast(I32), xs_picked[16 + b : P : 32, :].bitcast(I32))
 
         w1_bf = keep.tile([P, PACK * H], BF16, name="w1_bf", align_bytes=64)
         cast_out = w1_bf[:].rearrange("p (t m j) -> p m t j", t=PACK, j=PACK)
@@ -94,6 +85,11 @@ def tile_picked_permun_gelu_po_kernel(
         nc.vector.tensor_copy(
             w2w[:].rearrange("p (t m b) -> p t m b", t=PACK, b=2),
             w2w_raw[:].rearrange("p (m t b) -> p t m b", t=PACK, b=2),
+        )
+
+        w2s = shared.tile([P, N], U8, name="w2s", align_bytes=64, offset=2 * N)
+        nc.vector.tensor_copy(
+            w2s[:].rearrange("p (t m) -> p t m", t=PACK), w2s_raw[:].rearrange("p (m t) -> p t m", t=PACK)
         )
 
         act = [keep.tile([P, S], F32, name="act%d" % t, align_bytes=64) for t in range(PACK)]

@@ -32,27 +32,23 @@ def tile_picked_permun_gelu_po_kernel(
 
         offs_sb = keep.tile([P, S // 16], U16, name="offs_sb")
         back_sb = keep.tile([P, S // 16], U16, name="back_sb")
-        xs_all = keep.tile([P, T], U8, name="xs_all", align_bytes=64)
         xs_mm = keep.tile([P, S], U8, name="xs_mm", align_bytes=64)
         w1_raw = keep.tile([P, PACK, H], F32, name="w1_raw", align_bytes=64)
         xw_all = shared.tile([P, T], I32, name="xw_all", align_bytes=64, offset=0)
         w2w_raw = shared.tile([P, 2 * N], U8, name="w2w_raw", align_bytes=64, offset=4 * T)
-        w2s_raw = shared.tile([P, N], U8, name="w2s_raw", align_bytes=64, offset=4 * T + 2 * N)
+        xs_all = shared.tile([P, T], U8, name="xs_all", align_bytes=64, offset=4 * T + 2 * N)
 
         nc.vector.memset(xs_all[:].bitcast(I32), 0)
-        nc.gpsimd.memset(w2s_raw[:].bitcast(I32), 0)
 
+        w1_rows = w1.rearrange("(p j) c -> p j c", j=PACK)
         nc.sync.dma_start(offs_sb[:], offs)
+        nc.sync.dma_start(back_sb[:], back)
+        nc.sync.dma_start(w1_raw[:, 0:1, :], w1_rows[:, 0:1, :])
         for b in range(2):
-            nc.scalar.dma_start(xs_all[b:P:16, :].bitcast(I32), x_scales[0, b:16:2, :].bitcast(I32))
-        nc.sync.dma_start(w1_raw[:], w1.rearrange("(p j) c -> p j c", j=PACK))
+            nc.sync.dma_start(xs_all[b:P:16, :].bitcast(I32), x_scales[0, b:16:2, :].bitcast(I32))
+        nc.sync.dma_start(w1_raw[:, 1:4, :], w1_rows[:, 1:4, :])
         nc.sync.dma_start(xw_all[:], x_words[0].rearrange("p n r -> p (n r)").bitcast(I32))
         nc.sync.dma_start(w2w_raw[:].bitcast(I32), w2_words[0].bitcast(I32))
-        nc.sync.dma_start(back_sb[:], back)
-        for q in range(4):
-            nc.gpsimd.dma_start(
-                w2s_raw[32 * q : 32 * q + 4, :].bitcast(I32), w2_scales[0, 4 * q : 4 * q + 4, :].bitcast(I32)
-            )
 
         xs_picked = keep.tile([P, S], U8, name="xs_picked", align_bytes=64)
         nc.vector.tensor_copy(xs_picked[:], xs_all[:].indirect(offs_sb[:]))
@@ -60,11 +56,18 @@ def tile_picked_permun_gelu_po_kernel(
         for b in range(2):
             nc.scalar.dma_start(xs_mm[2 + b : P : 32, :].bitcast(I32), xs_picked[16 + b : P : 32, :].bitcast(I32))
 
+        w2s_raw = shared.tile([P, N], U8, name="w2s_raw", align_bytes=64, offset=4 * T + 2 * N)
+        nc.vector.memset(w2s_raw[:].bitcast(I32), 0)
+        for q in range(4):
+            nc.sync.dma_start(
+                w2s_raw[32 * q : 32 * q + 4, :].bitcast(I32), w2_scales[0, 4 * q : 4 * q + 4, :].bitcast(I32)
+            )
+
         w1_bf = keep.tile([P, PACK * H], BF16, name="w1_bf", align_bytes=64)
-        cast_out = w1_bf[:].rearrange("p (t m j) -> p m t j", t=PACK, j=PACK)
-        cast_in = w1_raw[:].rearrange("p j (m t) -> p m t j", t=PACK)
+        cast_out = w1_bf[:].rearrange("p (t m j) -> p m j t", t=PACK, j=PACK)
+        cast_in = w1_raw[:].rearrange("p j (m t) -> p m j t", t=PACK)
         for pair in range(2):
-            nc.vector.tensor_copy(cast_out[:, :, 2 * pair : 2 * pair + 2], cast_in[:, :, 2 * pair : 2 * pair + 2])
+            nc.vector.tensor_copy(cast_out[:, :, :, 2 * pair : 2 * pair + 2], cast_in[:, :, :, 2 * pair : 2 * pair + 2])
         w1_codes = keep.tile([P, H], U32, name="w1_codes", align_bytes=64)
         w1_scale = keep.tile([P, H], U8, name="w1_scale", align_bytes=64)
         for pair in range(2):
@@ -75,32 +78,31 @@ def tile_picked_permun_gelu_po_kernel(
                 w1_bf[:, 2 * P * PACK * pair : 2 * P * PACK * (pair + 1)],
             )
 
-        xw = []
+        xw = keep.tile([P, S], U32, name="xw_picked", align_bytes=64)
         for h in range(2):
-            picked = keep.tile([P, HALF], U32, name="xw_picked%d" % h, align_bytes=64)
-            nc.vector.tensor_copy(picked[:], xw_all[:].bitcast(U32).indirect(offs_sb[:, 16 * h : 16 * h + 16]))
-            xw.append(picked)
+            nc.vector.tensor_copy(
+                xw[:, HALF * h : HALF * (h + 1)], xw_all[:].bitcast(U32).indirect(offs_sb[:, 16 * h : 16 * h + 16])
+            )
 
         w2w = shared.tile([P, 2 * N], U8, name="w2w", align_bytes=64, offset=0)
         nc.vector.tensor_copy(
-            w2w[:].rearrange("p (t m b) -> p t m b", t=PACK, b=2),
-            w2w_raw[:].rearrange("p (m t b) -> p t m b", t=PACK, b=2),
+            w2w[:].bitcast(U16).rearrange("p (t m) -> p m t", t=PACK),
+            w2w_raw[:].bitcast(U16).rearrange("p (m t) -> p m t", t=PACK),
         )
-
         w2s = shared.tile([P, N], U8, name="w2s", align_bytes=64, offset=2 * N)
         nc.vector.tensor_copy(
-            w2s[:].rearrange("p (t m) -> p t m", t=PACK), w2s_raw[:].rearrange("p (m t) -> p t m", t=PACK)
+            w2s[:].rearrange("p (t m) -> p m t", t=PACK), w2s_raw[:].rearrange("p (m t) -> p m t", t=PACK)
         )
 
         act = [keep.tile([P, S], F32, name="act%d" % t, align_bytes=64) for t in range(PACK)]
-        for t, h in [(0, 0), (1, 0), (0, 1), (1, 1), (2, 0), (2, 1), (3, 0), (3, 1)]:
-            bank = psum.tile([P, HALF], F32, name="y_bank", tag="bank")
-            cols = slice(HALF * h, HALF * (h + 1))
+        low, high, whole = slice(0, HALF), slice(HALF, S), slice(0, S)
+        for t, cols in [(0, low), (1, low), (0, high), (1, high), (2, whole), (3, whole)]:
+            bank = psum.tile([P, cols.stop - cols.start], F32, name="y_bank", tag="bank")
             nc.tensor.matmul_mx(
                 bank[:],
                 lhsT=w1_codes[:, P * t : P * (t + 1)].bitcast(FP8X4),
                 lhsT_scale=w1_scale[:, P * t : P * (t + 1)],
-                rhs=xw[h][:].bitcast(FP8X4),
+                rhs=xw[:, cols].bitcast(FP8X4),
                 rhs_scale=xs_mm[:, cols],
                 start=True,
                 stop=True,
@@ -112,23 +114,22 @@ def tile_picked_permun_gelu_po_kernel(
         out_codes = keep.tile([P, S], U32, name="out_codes", align_bytes=64)
         out_scale = keep.tile([P, S], U8, name="out_scale", align_bytes=64)
 
-        def fetch(planes, ts, first, width):
-            for slot, t in enumerate(ts):
+        def fetch(planes, first, width):
+            for t in range(PACK):
                 nc.vector.tensor_copy(
-                    planes[:, slot, :], act[t][:].indirect(back_sb[:, first // 16 : (first + width) // 16])
+                    planes[:, t, :], act[t][:].indirect(back_sb[:, first // 16 : (first + width) // 16])
                 )
 
-        def weave(planes, name, engine_copy):
-            woven = keep.tile([P, planes.shape[2], PACK], BF16, name=name, tag=name, align_bytes=64)
-            engine_copy(woven[:], planes.rearrange("p t n -> p n t"))
-            return woven
+        def weave(engine_copy, woven, planes):
+            engine_copy(woven.rearrange("p (c i) t -> p c t i", i=4), planes.rearrange("p t (c i) -> p c t i", i=4))
 
-        def second_product(woven, c, banks):
-            z_codes = keep.tile([P, CHUNK], U32, name="z_codes%d" % c, align_bytes=64)
-            z_scale = keep.tile([P, CHUNK], U8, name="z_scale%d" % c, align_bytes=64)
+        def quantize_z(z_codes, z_scale, woven):
             nc.vector.quantize_mx(z_codes[:].bitcast(FP8X4), z_scale[:], woven.rearrange("p n t -> p (n t)"))
+
+        def second_product(z_codes, z_scale, banks):
             per_bank = PACK // banks
-            tiles = [psum.tile([P, per_bank, CHUNK], F32, name="out_bank", tag="bank") for b in range(banks)]
+            width = z_codes.shape[1]
+            tiles = [psum.tile([P, per_bank, width], F32, name="out_bank", tag="bank") for b in range(banks)]
             for t in range(PACK):
                 nc.tensor.matmul_mx(
                     tiles[t // per_bank][:, t % per_bank, :],
@@ -141,59 +142,67 @@ def tile_picked_permun_gelu_po_kernel(
                 )
             return tiles
 
-        def columns(c):
-            return slice(CHUNK * c, CHUNK * (c + 1))
-
-        result = [keep.tile([P, PACK, CHUNK], F32, name="result%d" % c, align_bytes=64) for c in range(4)]
-        rounded = [keep.tile([P, CHUNK, PACK], BF16, name="rounded%d" % c, align_bytes=64) for c in range(4)]
-
-        def store_result(banks, c):
-            for bank, ts in banks:
-                nc.scalar.copy(result[c][:, ts, :], bank[:])
-            nc.sync.dma_start(out_rows[:, :, columns(c)], result[c][:])
-
-        def round_result(c):
-            nc.vector.tensor_copy(rounded[c][:], result[c][:].rearrange("p t n -> p n t"))
-
-        def quantize_result(c):
+        def quantize_result(rounded, cols):
             nc.vector.quantize_mx(
-                out_codes[:, columns(c)].bitcast(FP8X4),
-                out_scale[:, columns(c)],
-                rounded[c][:].rearrange("p n t -> p (n t)"),
+                out_codes[:, cols].bitcast(FP8X4), out_scale[:, cols], rounded[:].rearrange("p n t -> p (n t)")
             )
 
-        fetched = shared.tile([P, CHUNK + 2 * PACK * CHUNK], BF16, name="fetched", align_bytes=64, offset=4 * T)
-        planes01 = fetched[:, CHUNK:].rearrange("p (t n) -> p t n", t=PACK)
-        planes2 = fetched[:, : PACK * CHUNK].rearrange("p (t n) -> p t n", t=PACK)
-        planes3 = fetched[:, PACK * CHUNK : 2 * PACK * CHUNK].rearrange("p (t n) -> p t n", t=PACK)
-        fetch(planes01, range(PACK), 0, 2 * CHUNK)
-        woven01 = keep.tile([P, 2 * CHUNK, PACK], BF16, name="woven01", align_bytes=64)
-        nc.scalar.copy(woven01[:, :, 0:2], planes01[:, 0:2, :].rearrange("p t n -> p n t"))
-        for c in range(2):
-            nc.scalar.copy(woven01[:, columns(c), 2:4], planes01[:, 2:4, columns(c)].rearrange("p t n -> p n t"))
-        fetch(planes2, range(PACK), 2 * CHUNK, CHUNK)
-        (bank0,) = second_product(woven01[:, :CHUNK, :], 0, 1)
-        (bank1,) = second_product(woven01[:, CHUNK:, :], 1, 1)
-        woven2 = weave(planes2, "woven2", nc.scalar.copy)
-        fetch(planes3, range(PACK), 3 * CHUNK, CHUNK)
-        (bank2,) = second_product(woven2[:], 2, 1)
-        woven3 = weave(planes3, "woven3", nc.vector.tensor_copy)
-        low, high = second_product(woven3[:], 3, 2)
+        cols_a, cols_b, cols_c = slice(0, HALF), slice(HALF, HALF + CHUNK), slice(HALF + CHUNK, S)
+        fetched = shared.tile([P, PACK * HALF], BF16, name="fetched", align_bytes=64, offset=4 * T)
+        planes_a = fetched[:].rearrange("p (t n) -> p t n", t=PACK)
+        planes_b = fetched[:, : PACK * CHUNK].rearrange("p (t n) -> p t n", t=PACK)
+        woven_ab = keep.tile([P, PACK * (HALF + CHUNK)], BF16, name="woven_ab", align_bytes=64)
+        woven_a = woven_ab[:, : PACK * HALF].rearrange("p (n t) -> p n t", t=PACK)
+        woven_b = woven_ab[:, PACK * HALF :].rearrange("p (n t) -> p n t", t=PACK)
+        planes_c = woven_ab[:, PACK * HALF - 2 * CHUNK : PACK * HALF + 2 * CHUNK].rearrange("p (t n) -> p t n", t=PACK)
 
-        every_t = slice(0, PACK)
-        for c, bank in enumerate([bank0, bank1]):
-            store_result([(bank, every_t)], c)
-            round_result(c)
-        quantize_result(0)
-        quantize_result(1)
-        nc.sync.dma_start(out_words[:, :HALF], out_codes[:, :HALF].bitcast(I32))
-        store_result([(bank2, every_t)], 2)
-        round_result(2)
-        store_result([(low, slice(0, 2)), (high, slice(2, 4))], 3)
-        round_result(3)
-        quantize_result(2)
-        quantize_result(3)
-        nc.sync.dma_start(out_words[:, HALF:], out_codes[:, HALF:].bitcast(I32))
+        fetch(planes_a, 0, HALF)
+        weave(nc.scalar.copy, woven_a[:, :, 0:2], planes_a[:, 0:2, :])
+        weave(nc.scalar.copy, woven_a[:, :, 2:4], planes_a[:, 2:4, :])
+        fetch(planes_b, HALF, CHUNK)
+        z_codes_a = keep.tile([P, HALF], U32, name="z_codes_a", align_bytes=64)
+        z_scale_a = keep.tile([P, HALF], U8, name="z_scale_a", align_bytes=64)
+        quantize_z(z_codes_a, z_scale_a, woven_a)
+        banks_a = second_product(z_codes_a, z_scale_a, 2)
+        weave(nc.scalar.copy, woven_b, planes_b)
+        z_codes_b = keep.tile([P, CHUNK], U32, name="z_codes_b", align_bytes=64)
+        z_scale_b = keep.tile([P, CHUNK], U8, name="z_scale_b", align_bytes=64)
+        quantize_z(z_codes_b, z_scale_b, woven_b)
+        banks_b = second_product(z_codes_b, z_scale_b, 1)
+        fetch(planes_c, HALF + CHUNK, CHUNK)
+        woven_c = keep.tile([P, CHUNK, PACK], BF16, name="woven_c", align_bytes=64)
+        weave(nc.vector.tensor_copy, woven_c[:], planes_c)
+        z_codes_c = keep.tile([P, CHUNK], U32, name="z_codes_c", align_bytes=64)
+        z_scale_c = keep.tile([P, CHUNK], U8, name="z_scale_c", align_bytes=64)
+        quantize_z(z_codes_c, z_scale_c, woven_c[:])
+        banks_c = second_product(z_codes_c, z_scale_c, 2)
+
+        result_a = keep.tile([P, PACK, HALF], F32, name="result_a", align_bytes=64)
+        result_b = keep.tile([P, PACK, CHUNK], F32, name="result_b", align_bytes=64)
+        result_c = keep.tile([P, PACK, CHUNK], F32, name="result_c", align_bytes=64)
+        rounded_a = keep.tile([P, HALF, PACK], BF16, name="rounded_a", align_bytes=64)
+        rounded_b = keep.tile([P, CHUNK, PACK], BF16, name="rounded_b", align_bytes=64)
+        rounded_c = keep.tile([P, CHUNK, PACK], BF16, name="rounded_c", align_bytes=64)
+
+        for pair in range(2):
+            ts = slice(2 * pair, 2 * pair + 2)
+            nc.scalar.copy(result_a[:, ts, :], banks_a[pair][:])
+            nc.sync.dma_start(out_rows[:, ts, cols_a], result_a[:, ts, :])
+        nc.scalar.copy(result_b[:], banks_b[0][:])
+        nc.sync.dma_start(out_rows[:, :, cols_b], result_b[:])
+        weave(nc.scalar.copy, rounded_a[:, :CHUNK, :], result_a[:, :, :CHUNK])
+        weave(nc.vector.tensor_copy, rounded_a[:, CHUNK:, :], result_a[:, :, CHUNK:])
+        weave(nc.vector.tensor_copy, rounded_b[:], result_b[:])
+        quantize_result(rounded_a, cols_a)
+        nc.sync.dma_start(out_words[:, cols_a], out_codes[:, cols_a].bitcast(I32))
+        quantize_result(rounded_b, cols_b)
+        for pair in range(2):
+            ts = slice(2 * pair, 2 * pair + 2)
+            nc.scalar.copy(result_c[:, ts, :], banks_c[pair][:])
+        nc.sync.dma_start(out_rows[:, :, cols_c], result_c[:])
+        weave(nc.vector.tensor_copy, rounded_c[:], result_c[:])
+        quantize_result(rounded_c, cols_c)
+        nc.sync.dma_start(out_words[:, high], out_codes[:, high].bitcast(I32))
 
         out_scale_rows = out_2[0].bitcast(I32)
         for q in range(4):

@@ -19,6 +19,7 @@ P = 128
 PACK = 4
 HALF = S // 2
 CHUNK = 128
+FRONT = 768
 
 
 def tile_picked_permun_gelu_po_kernel(
@@ -40,13 +41,14 @@ def tile_picked_permun_gelu_po_kernel(
 
         nc.vector.memset(xs_all[:].bitcast(I32), 0)
 
-        w1_rows = w1.rearrange("(p j) c -> p j c", j=PACK)
+        w1_rows = w1.rearrange("(p j) c -> p (j c)", j=PACK)
+        w1_flat = w1_raw[:].rearrange("p j c -> p (j c)")
+        nc.sync.dma_start(w1_flat[:, :FRONT], w1_rows[:, :FRONT])
         nc.sync.dma_start(offs_sb[:], offs)
         nc.sync.dma_start(back_sb[:], back)
-        nc.sync.dma_start(w1_raw[:, 0:1, :], w1_rows[:, 0:1, :])
         for b in range(2):
             nc.sync.dma_start(xs_all[b:P:16, :].bitcast(I32), x_scales[0, b:16:2, :].bitcast(I32))
-        nc.sync.dma_start(w1_raw[:, 1:4, :], w1_rows[:, 1:4, :])
+        nc.sync.dma_start(w1_flat[:, FRONT:], w1_rows[:, FRONT:])
         nc.sync.dma_start(xw_all[:], x_words[0].rearrange("p n r -> p (n r)").bitcast(I32))
         nc.sync.dma_start(w2w_raw[:].bitcast(I32), w2_words[0].bitcast(I32))
 
@@ -57,7 +59,7 @@ def tile_picked_permun_gelu_po_kernel(
             nc.scalar.dma_start(xs_mm[2 + b : P : 32, :].bitcast(I32), xs_picked[16 + b : P : 32, :].bitcast(I32))
 
         w2s_raw = shared.tile([P, N], U8, name="w2s_raw", align_bytes=64, offset=4 * T + 2 * N)
-        nc.vector.memset(w2s_raw[:].bitcast(I32), 0)
+        nc.gpsimd.memset(w2s_raw[:].bitcast(I32), 0)
         for q in range(4):
             nc.sync.dma_start(
                 w2s_raw[32 * q : 32 * q + 4, :].bitcast(I32), w2_scales[0, 4 * q : 4 * q + 4, :].bitcast(I32)

@@ -88,12 +88,12 @@ def tile_picked_permun_gelu_po_kernel(
 
         w2w = shared.tile([P, 2 * N], U8, name="w2w", align_bytes=64, offset=0)
         nc.vector.tensor_copy(
-            w2w[:].bitcast(U16).rearrange("p (t m) -> p m t", t=PACK),
-            w2w_raw[:].bitcast(U16).rearrange("p (m t) -> p m t", t=PACK),
+            w2w[:].bitcast(U16).rearrange("p (t m) -> p t m", t=PACK),
+            w2w_raw[:].bitcast(U16).rearrange("p (m t) -> p t m", t=PACK),
         )
         w2s = shared.tile([P, N], U8, name="w2s", align_bytes=64, offset=2 * N)
         nc.vector.tensor_copy(
-            w2s[:].rearrange("p (t m) -> p m t", t=PACK), w2s_raw[:].rearrange("p (m t) -> p m t", t=PACK)
+            w2s[:].rearrange("p (t m) -> p t m", t=PACK), w2s_raw[:].rearrange("p (m t) -> p t m", t=PACK)
         )
 
         act = [keep.tile([P, S], F32, name="act%d" % t, align_bytes=64) for t in range(PACK)]
@@ -153,23 +153,23 @@ def tile_picked_permun_gelu_po_kernel(
         fetched = shared.tile([P, PACK * HALF], BF16, name="fetched", align_bytes=64, offset=4 * T)
         planes_a = fetched[:].rearrange("p (t n) -> p t n", t=PACK)
         planes_b = fetched[:, : PACK * CHUNK].rearrange("p (t n) -> p t n", t=PACK)
-        woven_ab = keep.tile([P, PACK * (HALF + CHUNK)], BF16, name="woven_ab", align_bytes=64)
-        woven_a = woven_ab[:, : PACK * HALF].rearrange("p (n t) -> p n t", t=PACK)
-        woven_b = woven_ab[:, PACK * HALF :].rearrange("p (n t) -> p n t", t=PACK)
-        planes_c = woven_ab[:, PACK * HALF - 2 * CHUNK : PACK * HALF + 2 * CHUNK].rearrange("p (t n) -> p t n", t=PACK)
+        planes_c = fetched[:, 2 * CHUNK : 6 * CHUNK].rearrange("p (t n) -> p t n", t=PACK)
+        woven_a = keep.tile([P, HALF, PACK], BF16, name="woven_a", align_bytes=64)
+        woven_b = keep.tile([P, CHUNK, PACK], BF16, name="woven_b", align_bytes=64)
 
         fetch(planes_a, 0, HALF)
-        weave(nc.scalar.copy, woven_a[:, :, 0:2], planes_a[:, 0:2, :])
+        for cols in (slice(0, CHUNK), slice(CHUNK, HALF)):
+            weave(nc.scalar.copy, woven_a[:, cols, 0:2], planes_a[:, 0:2, cols])
         weave(nc.scalar.copy, woven_a[:, :, 2:4], planes_a[:, 2:4, :])
         fetch(planes_b, HALF, CHUNK)
         z_codes_a = keep.tile([P, HALF], U32, name="z_codes_a", align_bytes=64)
         z_scale_a = keep.tile([P, HALF], U8, name="z_scale_a", align_bytes=64)
-        quantize_z(z_codes_a, z_scale_a, woven_a)
+        quantize_z(z_codes_a, z_scale_a, woven_a[:])
         banks_a = second_product(z_codes_a, z_scale_a, 2)
-        weave(nc.scalar.copy, woven_b, planes_b)
+        weave(nc.scalar.copy, woven_b[:], planes_b)
         z_codes_b = keep.tile([P, CHUNK], U32, name="z_codes_b", align_bytes=64)
         z_scale_b = keep.tile([P, CHUNK], U8, name="z_scale_b", align_bytes=64)
-        quantize_z(z_codes_b, z_scale_b, woven_b)
+        quantize_z(z_codes_b, z_scale_b, woven_b[:])
         banks_b = second_product(z_codes_b, z_scale_b, 1)
         fetch(planes_c, HALF + CHUNK, CHUNK)
         woven_c = keep.tile([P, CHUNK, PACK], BF16, name="woven_c", align_bytes=64)

@@ -97,11 +97,11 @@ def tile_picked_permun_gelu_po_kernel(
         )
 
         act = [keep.tile([P, S], F32, name="act%d" % t, align_bytes=64) for t in range(PACK)]
-        low, high, whole = slice(0, HALF), slice(HALF, S), slice(0, S)
-        for t, cols in [(0, low), (1, low), (0, high), (1, high), (2, whole), (3, whole)]:
-            bank = psum.tile([P, cols.stop - cols.start], F32, name="y_bank", tag="bank")
+        low, high = slice(0, HALF), slice(HALF, S)
+        for t, cols in [(0, low), (1, low), (0, high), (1, high), (2, low), (2, high), (3, low), (3, high)]:
+            bank = psum.tile([P, S], F32, name="y_bank", tag="bank")
             nc.tensor.matmul_mx(
-                bank[:],
+                bank[:, cols],
                 lhsT=w1_codes[:, P * t : P * (t + 1)].bitcast(FP8X4),
                 lhsT_scale=w1_scale[:, P * t : P * (t + 1)],
                 rhs=xw[:, cols].bitcast(FP8X4),
@@ -109,7 +109,17 @@ def tile_picked_permun_gelu_po_kernel(
                 start=True,
                 stop=True,
             )
-            nc.scalar.activation(act[t][:, cols], bank[:], GELU)
+            nc.scalar.activation(act[t][:, cols], bank[:, cols], GELU)
+        for t in range(2):
+            nc.tensor.matmul_mx(
+                bank[:],
+                lhsT=w1_codes[:, P * t : P * (t + 1)].bitcast(FP8X4),
+                lhsT_scale=w1_scale[:, P * t : P * (t + 1)],
+                rhs=xw[:].bitcast(FP8X4),
+                rhs_scale=xs_mm[:],
+                start=True,
+                stop=True,
+            )
 
         out_rows = out_0.rearrange("(p t) j -> p t j", t=PACK)
         out_words = out_1[0].rearrange("p n r -> p (n r)").bitcast(I32)

@@ -46,8 +46,7 @@ def tile_picked_permun_gelu_po_kernel(
         nc.sync.dma_start(w1_flat[:, :FRONT], w1_rows[:, :FRONT])
         nc.sync.dma_start(offs_sb[:], offs)
         nc.sync.dma_start(back_sb[:], back)
-        for b in range(2):
-            nc.sync.dma_start(xs_all[b:P:16, :].bitcast(I32), x_scales[0, b:16:2, :].bitcast(I32))
+        nc.sync.dma_start(xs_all[0:P:8, :].bitcast(I32), x_scales[0].bitcast(I32))
         nc.sync.dma_start(w1_flat[:, FRONT:], w1_rows[:, FRONT:])
         nc.sync.dma_start(xw_all[:], x_words[0].rearrange("p n r -> p (n r)").bitcast(I32))
         nc.sync.dma_start(w2w_raw[:].bitcast(I32), w2_words[0].bitcast(I32))
@@ -55,8 +54,8 @@ def tile_picked_permun_gelu_po_kernel(
         xs_picked = keep.tile([P, S], U8, name="xs_picked", align_bytes=64)
         nc.vector.tensor_copy(xs_picked[:], xs_all[:].indirect(offs_sb[:]))
         nc.vector.tensor_copy(xs_mm[:].bitcast(I32), xs_picked[:].bitcast(I32))
-        for b in range(2):
-            nc.scalar.dma_start(xs_mm[2 + b : P : 32, :].bitcast(I32), xs_picked[16 + b : P : 32, :].bitcast(I32))
+        for r in range(1, 4):
+            nc.scalar.dma_start(xs_mm[r:P:32, :].bitcast(I32), xs_picked[8 * r : P : 32, :].bitcast(I32))
 
         w2s_raw = shared.tile([P, N], U8, name="w2s_raw", align_bytes=64, offset=4 * T + 2 * N)
         nc.gpsimd.memset(w2s_raw[:].bitcast(I32), 0)
@@ -97,11 +96,11 @@ def tile_picked_permun_gelu_po_kernel(
         )
 
         act = [keep.tile([P, S], F32, name="act%d" % t, align_bytes=64) for t in range(PACK)]
-        low, high = slice(0, HALF), slice(HALF, S)
-        for t, cols in [(0, low), (1, low), (0, high), (1, high), (2, low), (2, high), (3, low), (3, high)]:
-            bank = psum.tile([P, S], F32, name="y_bank", tag="bank")
+        low, high, whole = slice(0, HALF), slice(HALF, S), slice(0, S)
+        for t, cols in [(0, low), (1, low), (0, high), (1, high), (2, whole), (3, whole)]:
+            bank = psum.tile([P, cols.stop - cols.start], F32, name="y_bank", tag="bank")
             nc.tensor.matmul_mx(
-                bank[:, cols],
+                bank[:],
                 lhsT=w1_codes[:, P * t : P * (t + 1)].bitcast(FP8X4),
                 lhsT_scale=w1_scale[:, P * t : P * (t + 1)],
                 rhs=xw[:, cols].bitcast(FP8X4),
@@ -109,17 +108,7 @@ def tile_picked_permun_gelu_po_kernel(
                 start=True,
                 stop=True,
             )
-            nc.scalar.activation(act[t][:, cols], bank[:, cols], GELU)
-        for t in range(2):
-            nc.tensor.matmul_mx(
-                bank[:],
-                lhsT=w1_codes[:, P * t : P * (t + 1)].bitcast(FP8X4),
-                lhsT_scale=w1_scale[:, P * t : P * (t + 1)],
-                rhs=xw[:].bitcast(FP8X4),
-                rhs_scale=xs_mm[:],
-                start=True,
-                stop=True,
-            )
+            nc.scalar.activation(act[t][:, cols], bank[:], GELU)
 
         out_rows = out_0.rearrange("(p t) j -> p t j", t=PACK)
         out_words = out_1[0].rearrange("p n r -> p (n r)").bitcast(I32)
@@ -206,15 +195,15 @@ def tile_picked_permun_gelu_po_kernel(
         weave(nc.vector.tensor_copy, rounded_a[:, CHUNK:, :], result_a[:, :, CHUNK:])
         weave(nc.vector.tensor_copy, rounded_b[:], result_b[:])
         quantize_result(rounded_a, cols_a)
-        nc.sync.dma_start(out_words[:, cols_a], out_codes[:, cols_a].bitcast(I32))
         quantize_result(rounded_b, cols_b)
+        nc.sync.dma_start(out_words[:, : cols_b.stop], out_codes[:, : cols_b.stop].bitcast(I32))
         for pair in range(2):
             ts = slice(2 * pair, 2 * pair + 2)
             nc.scalar.copy(result_c[:, ts, :], banks_c[pair][:])
         nc.sync.dma_start(out_rows[:, :, cols_c], result_c[:])
         weave(nc.vector.tensor_copy, rounded_c[:], result_c[:])
         quantize_result(rounded_c, cols_c)
-        nc.sync.dma_start(out_words[:, high], out_codes[:, high].bitcast(I32))
+        nc.sync.dma_start(out_words[:, cols_c], out_codes[:, cols_c].bitcast(I32))
 
         out_scale_rows = out_2[0].bitcast(I32)
         for q in range(4):

@@ -97,10 +97,9 @@ def tile_picked_permun_gelu_po_kernel(
 
         act = [keep.tile([P, S], F32, name="act%d" % t, align_bytes=64) for t in range(PACK)]
         low, high, whole = slice(0, HALF), slice(HALF, S), slice(0, S)
-        for t, cols in [(0, low), (1, low), (0, high), (1, high), (2, whole), (3, whole)]:
-            bank = psum.tile([P, cols.stop - cols.start], F32, name="y_bank", tag="bank")
+        def first_product(bank, t, cols):
             nc.tensor.matmul_mx(
-                bank[:],
+                bank[:, cols],
                 lhsT=w1_codes[:, P * t : P * (t + 1)].bitcast(FP8X4),
                 lhsT_scale=w1_scale[:, P * t : P * (t + 1)],
                 rhs=xw[:, cols].bitcast(FP8X4),
@@ -108,17 +107,29 @@ def tile_picked_permun_gelu_po_kernel(
                 start=True,
                 stop=True,
             )
-            nc.scalar.activation(act[t][:, cols], bank[:], GELU)
+
+        y_banks = [psum.tile([P, S], F32, name="y_bank", tag="bank") for b in range(6)]
+        first_product(y_banks[0], 0, low)
+        nc.scalar.activation(act[0][:, low], y_banks[0][:, low], GELU)
+        first_product(y_banks[1], 1, low)
+        for b, cols in ((2, slice(HALF, HALF + CHUNK)), (3, slice(HALF + CHUNK, S))):
+            first_product(y_banks[b], 0, cols)
+            nc.scalar.activation(act[0][:, cols], y_banks[b][:, cols], GELU)
+        first_product(y_banks[1], 1, high)
+        nc.scalar.activation(act[1][:], y_banks[1][:], GELU)
+        for t in (2, 3):
+            first_product(y_banks[2 + t], t, whole)
+            nc.scalar.activation(act[t][:], y_banks[2 + t][:], GELU)
 
         out_rows = out_0.rearrange("(p t) j -> p t j", t=PACK)
         out_words = out_1[0].rearrange("p n r -> p (n r)").bitcast(I32)
         out_codes = keep.tile([P, S], U32, name="out_codes", align_bytes=64)
         out_scale = keep.tile([P, S], U8, name="out_scale", align_bytes=64)
 
-        def fetch(planes, first, width):
-            for t in range(PACK):
+        def fetch(planes, first, width, order):
+            for t in order:
                 nc.vector.tensor_copy(
-                    planes[:, t, :], act[t][:].indirect(back_sb[:, first // 16 : (first + width) // 16])
+                    planes[t], act[t][:].indirect(back_sb[:, first // 16 : (first + width) // 16])
                 )
 
         def weave(engine_copy, woven, planes):
@@ -149,18 +160,21 @@ def tile_picked_permun_gelu_po_kernel(
             )
 
         cols_a, cols_b, cols_c = slice(0, HALF), slice(HALF, HALF + CHUNK), slice(HALF + CHUNK, S)
-        fetched = shared.tile([P, PACK * HALF], BF16, name="fetched", align_bytes=64, offset=4 * T)
-        planes_a = fetched[:].rearrange("p (t n) -> p t n", t=PACK)
-        planes_b = fetched[:, : PACK * CHUNK].rearrange("p (t n) -> p t n", t=PACK)
-        planes_c = fetched[:, 2 * CHUNK : 6 * CHUNK].rearrange("p (t n) -> p t n", t=PACK)
+        fetched = shared.tile([P, 9 * CHUNK], BF16, name="fetched", align_bytes=64, offset=4 * T)
+        pairs_a = [
+            fetched[:, 4 * CHUNK : 8 * CHUNK].rearrange("p (t n) -> p t n", t=2),
+            fetched[:, : 4 * CHUNK].rearrange("p (t n) -> p t n", t=2),
+        ]
+        planes_b = fetched[:, 5 * CHUNK :].rearrange("p (t n) -> p t n", t=PACK)
+        planes_c = fetched[:, : 8 * CHUNK].rearrange("p (t n) -> p t n", t=PACK)[:, :, CHUNK:]
         woven_a = keep.tile([P, HALF, PACK], BF16, name="woven_a", align_bytes=64)
         woven_b = keep.tile([P, CHUNK, PACK], BF16, name="woven_b", align_bytes=64)
 
-        fetch(planes_a, 0, HALF)
+        fetch([pairs_a[t // 2][:, t % 2, :] for t in range(PACK)], 0, HALF, range(PACK))
         for cols in (slice(0, CHUNK), slice(CHUNK, HALF)):
-            weave(nc.scalar.copy, woven_a[:, cols, 0:2], planes_a[:, 0:2, cols])
-        weave(nc.scalar.copy, woven_a[:, :, 2:4], planes_a[:, 2:4, :])
-        fetch(planes_b, HALF, CHUNK)
+            weave(nc.scalar.copy, woven_a[:, cols, 0:2], pairs_a[0][:, :, cols])
+        weave(nc.scalar.copy, woven_a[:, :, 2:4], pairs_a[1])
+        fetch([planes_b[:, t, :] for t in range(PACK)], HALF, CHUNK, (3, 1, 0, 2))
         z_codes_a = keep.tile([P, HALF], U32, name="z_codes_a", align_bytes=64)
         z_scale_a = keep.tile([P, HALF], U8, name="z_scale_a", align_bytes=64)
         quantize_z(z_codes_a, z_scale_a, woven_a[:])
@@ -170,7 +184,7 @@ def tile_picked_permun_gelu_po_kernel(
         z_scale_b = keep.tile([P, CHUNK], U8, name="z_scale_b", align_bytes=64)
         quantize_z(z_codes_b, z_scale_b, woven_b[:])
         banks_b = second_product(z_codes_b, z_scale_b, 1)
-        fetch(planes_c, HALF + CHUNK, CHUNK)
+        fetch([planes_c[:, t, :] for t in range(PACK)], HALF + CHUNK, CHUNK, range(PACK))
         woven_c = keep.tile([P, CHUNK, PACK], BF16, name="woven_c", align_bytes=64)
         weave(nc.vector.tensor_copy, woven_c[:], planes_c)
         z_codes_c = keep.tile([P, CHUNK], U32, name="z_codes_c", align_bytes=64)

@@ -20,6 +20,7 @@ PACK = 4
 HALF = S // 2
 CHUNK = 128
 FRONT = 768
+SHARE = 64
 
 
 def tile_picked_permun_gelu_po_kernel(
@@ -178,7 +179,7 @@ def tile_picked_permun_gelu_po_kernel(
         z_codes_a = keep.tile([P, HALF], U32, name="z_codes_a", align_bytes=64)
         z_scale_a = keep.tile([P, HALF], U8, name="z_scale_a", align_bytes=64)
         quantize_z(z_codes_a, z_scale_a, woven_a[:])
-        banks_a = second_product(z_codes_a, z_scale_a, 2)
+        banks_a = second_product(z_codes_a, z_scale_a, PACK)
         weave(nc.scalar.copy, woven_b[:], planes_b)
         z_codes_b = keep.tile([P, CHUNK], U32, name="z_codes_b", align_bytes=64)
         z_scale_b = keep.tile([P, CHUNK], U8, name="z_scale_b", align_bytes=64)
@@ -201,23 +202,25 @@ def tile_picked_permun_gelu_po_kernel(
 
         for pair in range(2):
             ts = slice(2 * pair, 2 * pair + 2)
-            nc.scalar.copy(result_a[:, ts, :], banks_a[pair][:])
+            for t in range(ts.start, ts.stop):
+                nc.scalar.copy(result_a[:, t : t + 1, :], banks_a[t][:])
             nc.sync.dma_start(out_rows[:, ts, cols_a], result_a[:, ts, :])
         nc.scalar.copy(result_b[:], banks_b[0][:])
         nc.sync.dma_start(out_rows[:, :, cols_b], result_b[:])
-        weave(nc.scalar.copy, rounded_a[:, :CHUNK, :], result_a[:, :, :CHUNK])
-        weave(nc.vector.tensor_copy, rounded_a[:, CHUNK:, :], result_a[:, :, CHUNK:])
+        weave(nc.scalar.copy, rounded_a[:, :SHARE, :], result_a[:, :, :SHARE])
+        weave(nc.vector.tensor_copy, rounded_a[:, SHARE:, :], result_a[:, :, SHARE:])
         weave(nc.vector.tensor_copy, rounded_b[:], result_b[:])
         quantize_result(rounded_a, cols_a)
+        nc.sync.dma_start(out_words[:, cols_a], out_codes[:, cols_a].bitcast(I32))
         quantize_result(rounded_b, cols_b)
-        nc.sync.dma_start(out_words[:, : cols_b.stop], out_codes[:, : cols_b.stop].bitcast(I32))
         for pair in range(2):
             ts = slice(2 * pair, 2 * pair + 2)
             nc.scalar.copy(result_c[:, ts, :], banks_c[pair][:])
         nc.sync.dma_start(out_rows[:, :, cols_c], result_c[:])
-        weave(nc.vector.tensor_copy, rounded_c[:], result_c[:])
+        for ts in (slice(0, 2), slice(2, 4)):
+            weave(nc.vector.tensor_copy, rounded_c[:, :, ts], result_c[:, ts, :])
         quantize_result(rounded_c, cols_c)
-        nc.sync.dma_start(out_words[:, cols_c], out_codes[:, cols_c].bitcast(I32))
+        nc.sync.dma_start(out_words[:, high], out_codes[:, high].bitcast(I32))
 
         out_scale_rows = out_2[0].bitcast(I32)
         for q in range(4):

@@ -17,10 +17,18 @@ GELU = mybir.ActivationFunctionType.Gelu_apprx_tanh
 
 P = 128
 PACK = 4
+LIST_ROWS = 16
+QUAD = 32
+BLOCK_ROWS = 8
 HALF = S // 2
 CHUNK = 128
-FRONT = 768
-SHARE = 64
+W1_FRONT = 768
+SCALAR_ROUNDS = 64
+BANKS = 8
+
+AT_WORDS = 0
+AT_W2_RAW = 4 * T
+AT_SCALES = AT_W2_RAW + 2 * N
 
 
 def tile_picked_permun_gelu_po_kernel(
@@ -30,74 +38,81 @@ def tile_picked_permun_gelu_po_kernel(
     with ExitStack() as ctx:
         keep = ctx.enter_context(tc.tile_pool(name="keep", bufs=1))
         shared = ctx.enter_context(tc.tile_pool(name="shared", bufs=1))
-        psum = ctx.enter_context(tc.psum_pool(name="psum", bufs=8))
+        psum = ctx.enter_context(tc.psum_pool(name="psum", bufs=BANKS))
 
-        offs_sb = keep.tile([P, S // 16], U16, name="offs_sb")
-        back_sb = keep.tile([P, S // 16], U16, name="back_sb")
+        offs_sb = keep.tile([P, S // LIST_ROWS], U16, name="offs_sb")
+        back_sb = keep.tile([P, S // LIST_ROWS], U16, name="back_sb")
         xs_mm = keep.tile([P, S], U8, name="xs_mm", align_bytes=64)
         w1_raw = keep.tile([P, PACK, H], F32, name="w1_raw", align_bytes=64)
-        xw_all = shared.tile([P, T], I32, name="xw_all", align_bytes=64, offset=0)
-        w2w_raw = shared.tile([P, 2 * N], U8, name="w2w_raw", align_bytes=64, offset=4 * T)
-        xs_all = shared.tile([P, T], U8, name="xs_all", align_bytes=64, offset=4 * T + 2 * N)
+        xw_all = shared.tile([P, T], I32, name="xw_all", align_bytes=64, offset=AT_WORDS)
+        w2w_raw = shared.tile([P, 2 * N], U8, name="w2w_raw", align_bytes=64, offset=AT_W2_RAW)
+        xs_all = shared.tile([P, T], U8, name="xs_all", align_bytes=64, offset=AT_SCALES)
 
         nc.vector.memset(xs_all[:].bitcast(I32), 0)
 
         w1_rows = w1.rearrange("(p j) c -> p (j c)", j=PACK)
         w1_flat = w1_raw[:].rearrange("p j c -> p (j c)")
-        nc.sync.dma_start(w1_flat[:, :FRONT], w1_rows[:, :FRONT])
+        nc.sync.dma_start(w1_flat[:, :W1_FRONT], w1_rows[:, :W1_FRONT])
         nc.sync.dma_start(offs_sb[:], offs)
         nc.sync.dma_start(back_sb[:], back)
-        nc.sync.dma_start(xs_all[0:P:8, :].bitcast(I32), x_scales[0].bitcast(I32))
-        nc.sync.dma_start(w1_flat[:, FRONT:], w1_rows[:, FRONT:])
+        nc.sync.dma_start(xs_all[0:P:BLOCK_ROWS, :].bitcast(I32), x_scales[0].bitcast(I32))
+        nc.sync.dma_start(w1_flat[:, W1_FRONT:], w1_rows[:, W1_FRONT:])
         nc.sync.dma_start(xw_all[:], x_words[0].rearrange("p n r -> p (n r)").bitcast(I32))
         nc.sync.dma_start(w2w_raw[:].bitcast(I32), w2_words[0].bitcast(I32))
 
         xs_picked = keep.tile([P, S], U8, name="xs_picked", align_bytes=64)
         nc.vector.tensor_copy(xs_picked[:], xs_all[:].indirect(offs_sb[:]))
         nc.vector.tensor_copy(xs_mm[:].bitcast(I32), xs_picked[:].bitcast(I32))
-        for r in range(1, 4):
-            nc.scalar.dma_start(xs_mm[r:P:32, :].bitcast(I32), xs_picked[8 * r : P : 32, :].bitcast(I32))
+        for r in range(1, PACK):
+            nc.scalar.dma_start(
+                xs_mm[r:P:QUAD, :].bitcast(I32), xs_picked[BLOCK_ROWS * r : P : QUAD, :].bitcast(I32)
+            )
 
-        w2s_raw = shared.tile([P, N], U8, name="w2s_raw", align_bytes=64, offset=4 * T + 2 * N)
+        w2s_raw = shared.tile([P, N], U8, name="w2s_raw", align_bytes=64, offset=AT_SCALES)
         nc.gpsimd.memset(w2s_raw[:].bitcast(I32), 0)
-        for q in range(4):
+        for q in range(P // QUAD):
             nc.sync.dma_start(
-                w2s_raw[32 * q : 32 * q + 4, :].bitcast(I32), w2_scales[0, 4 * q : 4 * q + 4, :].bitcast(I32)
+                w2s_raw[QUAD * q : QUAD * q + PACK, :].bitcast(I32),
+                w2_scales[0, PACK * q : PACK * (q + 1), :].bitcast(I32),
             )
 
         w1_bf = keep.tile([P, PACK * H], BF16, name="w1_bf", align_bytes=64)
         cast_out = w1_bf[:].rearrange("p (t m j) -> p m j t", t=PACK, j=PACK)
         cast_in = w1_raw[:].rearrange("p j (m t) -> p m j t", t=PACK)
-        for pair in range(2):
-            nc.vector.tensor_copy(cast_out[:, :, :, 2 * pair : 2 * pair + 2], cast_in[:, :, :, 2 * pair : 2 * pair + 2])
+        pairs = (slice(0, 2), slice(2, 4))
+        for ts in pairs:
+            nc.vector.tensor_copy(cast_out[:, :, :, ts], cast_in[:, :, :, ts])
         w1_codes = keep.tile([P, H], U32, name="w1_codes", align_bytes=64)
         w1_scale = keep.tile([P, H], U8, name="w1_scale", align_bytes=64)
-        for pair in range(2):
-            cols = slice(2 * P * pair, 2 * P * (pair + 1))
+        for ts in pairs:
+            dealt = slice(P * ts.start, P * ts.stop)
             nc.vector.quantize_mx(
-                w1_codes[:, cols].bitcast(FP8X4),
-                w1_scale[:, cols],
-                w1_bf[:, 2 * P * PACK * pair : 2 * P * PACK * (pair + 1)],
+                w1_codes[:, dealt].bitcast(FP8X4),
+                w1_scale[:, dealt],
+                w1_bf[:, PACK * dealt.start : PACK * dealt.stop],
             )
 
+        def entries(list_sb, cols):
+            return list_sb[:, cols.start // LIST_ROWS : cols.stop // LIST_ROWS]
+
+        low, high, whole = slice(0, HALF), slice(HALF, S), slice(0, S)
         xw = keep.tile([P, S], U32, name="xw_picked", align_bytes=64)
-        for h in range(2):
-            nc.vector.tensor_copy(
-                xw[:, HALF * h : HALF * (h + 1)], xw_all[:].bitcast(U32).indirect(offs_sb[:, 16 * h : 16 * h + 16])
-            )
+        for cols in (low, high):
+            nc.vector.tensor_copy(xw[:, cols], xw_all[:].bitcast(U32).indirect(entries(offs_sb, cols)))
 
-        w2w = shared.tile([P, 2 * N], U8, name="w2w", align_bytes=64, offset=0)
+        w2w = shared.tile([P, 2 * N], U8, name="w2w", align_bytes=64, offset=AT_WORDS)
         nc.vector.tensor_copy(
             w2w[:].bitcast(U16).rearrange("p (t m) -> p t m", t=PACK),
             w2w_raw[:].bitcast(U16).rearrange("p (m t) -> p t m", t=PACK),
         )
-        w2s = shared.tile([P, N], U8, name="w2s", align_bytes=64, offset=2 * N)
+        w2s = shared.tile([P, N], U8, name="w2s", align_bytes=64, offset=AT_WORDS + 2 * N)
         nc.vector.tensor_copy(
             w2s[:].rearrange("p (t m) -> p t m", t=PACK), w2s_raw[:].rearrange("p (m t) -> p t m", t=PACK)
         )
 
+        cols_a, cols_b, cols_c = low, slice(HALF, HALF + CHUNK), slice(HALF + CHUNK, S)
         act = [keep.tile([P, S], F32, name="act%d" % t, align_bytes=64) for t in range(PACK)]
-        low, high, whole = slice(0, HALF), slice(HALF, S), slice(0, S)
+
         def first_product(bank, t, cols):
             nc.tensor.matmul_mx(
                 bank[:, cols],
@@ -109,29 +124,32 @@ def tile_picked_permun_gelu_po_kernel(
                 stop=True,
             )
 
-        y_banks = [psum.tile([P, S], F32, name="y_bank", tag="bank") for b in range(6)]
-        first_product(y_banks[0], 0, low)
-        nc.scalar.activation(act[0][:, low], y_banks[0][:, low], GELU)
-        first_product(y_banks[1], 1, low)
-        for b, cols in ((2, slice(HALF, HALF + CHUNK)), (3, slice(HALF + CHUNK, S))):
-            first_product(y_banks[b], 0, cols)
-            nc.scalar.activation(act[0][:, cols], y_banks[b][:, cols], GELU)
-        first_product(y_banks[1], 1, high)
-        nc.scalar.activation(act[1][:], y_banks[1][:], GELU)
-        for t in (2, 3):
-            first_product(y_banks[2 + t], t, whole)
-            nc.scalar.activation(act[t][:], y_banks[2 + t][:], GELU)
+        def gelu(bank, t, cols):
+            nc.scalar.activation(act[t][:, cols], bank[:, cols], GELU)
+
+        bank_0_low, bank_1, bank_0_third, bank_0_fourth, bank_2, bank_3 = [
+            psum.tile([P, S], F32, name="y_bank", tag="bank") for b in range(PACK + 2)
+        ]
+        first_product(bank_0_low, 0, low)
+        gelu(bank_0_low, 0, low)
+        first_product(bank_1, 1, low)
+        for bank, cols in ((bank_0_third, cols_b), (bank_0_fourth, cols_c)):
+            first_product(bank, 0, cols)
+            gelu(bank, 0, cols)
+        first_product(bank_1, 1, high)
+        gelu(bank_1, 1, whole)
+        for bank, t in ((bank_2, 2), (bank_3, 3)):
+            first_product(bank, t, whole)
+            gelu(bank, t, whole)
 
         out_rows = out_0.rearrange("(p t) j -> p t j", t=PACK)
         out_words = out_1[0].rearrange("p n r -> p (n r)").bitcast(I32)
         out_codes = keep.tile([P, S], U32, name="out_codes", align_bytes=64)
         out_scale = keep.tile([P, S], U8, name="out_scale", align_bytes=64)
 
-        def fetch(planes, first, width, order):
+        def fetch(planes, cols, order):
             for t in order:
-                nc.vector.tensor_copy(
-                    planes[t], act[t][:].indirect(back_sb[:, first // 16 : (first + width) // 16])
-                )
+                nc.vector.tensor_copy(planes[t], act[t][:].indirect(entries(back_sb, cols)))
 
         def weave(engine_copy, woven, planes):
             engine_copy(woven.rearrange("p (c i) t -> p c t i", i=4), planes.rearrange("p t (c i) -> p c t i", i=4))
@@ -160,8 +178,7 @@ def tile_picked_permun_gelu_po_kernel(
                 out_codes[:, cols].bitcast(FP8X4), out_scale[:, cols], rounded[:].rearrange("p n t -> p (n t)")
             )
 
-        cols_a, cols_b, cols_c = slice(0, HALF), slice(HALF, HALF + CHUNK), slice(HALF + CHUNK, S)
-        fetched = shared.tile([P, 9 * CHUNK], BF16, name="fetched", align_bytes=64, offset=4 * T)
+        fetched = shared.tile([P, 9 * CHUNK], BF16, name="fetched", align_bytes=64, offset=AT_W2_RAW)
         pairs_a = [
             fetched[:, 4 * CHUNK : 8 * CHUNK].rearrange("p (t n) -> p t n", t=2),
             fetched[:, : 4 * CHUNK].rearrange("p (t n) -> p t n", t=2),
@@ -171,11 +188,11 @@ def tile_picked_permun_gelu_po_kernel(
         woven_a = keep.tile([P, HALF, PACK], BF16, name="woven_a", align_bytes=64)
         woven_b = keep.tile([P, CHUNK, PACK], BF16, name="woven_b", align_bytes=64)
 
-        fetch([pairs_a[t // 2][:, t % 2, :] for t in range(PACK)], 0, HALF, range(PACK))
-        for cols in (slice(0, CHUNK), slice(CHUNK, HALF)):
-            weave(nc.scalar.copy, woven_a[:, cols, 0:2], pairs_a[0][:, :, cols])
-        weave(nc.scalar.copy, woven_a[:, :, 2:4], pairs_a[1])
-        fetch([planes_b[:, t, :] for t in range(PACK)], HALF, CHUNK, (3, 1, 0, 2))
+        fetch([pairs_a[t // 2][:, t % 2, :] for t in range(PACK)], cols_a, range(PACK))
+        for part in (slice(0, CHUNK), slice(CHUNK, HALF)):
+            weave(nc.scalar.copy, woven_a[:, part, pairs[0]], pairs_a[0][:, :, part])
+        weave(nc.scalar.copy, woven_a[:, :, pairs[1]], pairs_a[1])
+        fetch([planes_b[:, t, :] for t in range(PACK)], cols_b, (3, 1, 0, 2))
         z_codes_a = keep.tile([P, HALF], U32, name="z_codes_a", align_bytes=64)
         z_scale_a = keep.tile([P, HALF], U8, name="z_scale_a", align_bytes=64)
         quantize_z(z_codes_a, z_scale_a, woven_a[:])
@@ -185,13 +202,13 @@ def tile_picked_permun_gelu_po_kernel(
         z_scale_b = keep.tile([P, CHUNK], U8, name="z_scale_b", align_bytes=64)
         quantize_z(z_codes_b, z_scale_b, woven_b[:])
         banks_b = second_product(z_codes_b, z_scale_b, 1)
-        fetch([planes_c[:, t, :] for t in range(PACK)], HALF + CHUNK, CHUNK, range(PACK))
+        fetch([planes_c[:, t, :] for t in range(PACK)], cols_c, range(PACK))
         woven_c = keep.tile([P, CHUNK, PACK], BF16, name="woven_c", align_bytes=64)
         weave(nc.vector.tensor_copy, woven_c[:], planes_c)
         z_codes_c = keep.tile([P, CHUNK], U32, name="z_codes_c", align_bytes=64)
         z_scale_c = keep.tile([P, CHUNK], U8, name="z_scale_c", align_bytes=64)
         quantize_z(z_codes_c, z_scale_c, woven_c[:])
-        banks_c = second_product(z_codes_c, z_scale_c, 2)
+        banks_c = second_product(z_codes_c, z_scale_c, PACK)
 
         result_a = keep.tile([P, PACK, HALF], F32, name="result_a", align_bytes=64)
         result_b = keep.tile([P, PACK, CHUNK], F32, name="result_b", align_bytes=64)
@@ -200,29 +217,29 @@ def tile_picked_permun_gelu_po_kernel(
         rounded_b = keep.tile([P, CHUNK, PACK], BF16, name="rounded_b", align_bytes=64)
         rounded_c = keep.tile([P, CHUNK, PACK], BF16, name="rounded_c", align_bytes=64)
 
-        for pair in range(2):
-            ts = slice(2 * pair, 2 * pair + 2)
+        for ts in pairs:
             for t in range(ts.start, ts.stop):
                 nc.scalar.copy(result_a[:, t : t + 1, :], banks_a[t][:])
             nc.sync.dma_start(out_rows[:, ts, cols_a], result_a[:, ts, :])
         nc.scalar.copy(result_b[:], banks_b[0][:])
         nc.sync.dma_start(out_rows[:, :, cols_b], result_b[:])
-        weave(nc.scalar.copy, rounded_a[:, :SHARE, :], result_a[:, :, :SHARE])
-        weave(nc.vector.tensor_copy, rounded_a[:, SHARE:, :], result_a[:, :, SHARE:])
+        weave(nc.scalar.copy, rounded_a[:, :SCALAR_ROUNDS, :], result_a[:, :, :SCALAR_ROUNDS])
+        weave(nc.vector.tensor_copy, rounded_a[:, SCALAR_ROUNDS:, :], result_a[:, :, SCALAR_ROUNDS:])
         weave(nc.vector.tensor_copy, rounded_b[:], result_b[:])
         quantize_result(rounded_a, cols_a)
         nc.sync.dma_start(out_words[:, cols_a], out_codes[:, cols_a].bitcast(I32))
         quantize_result(rounded_b, cols_b)
-        for pair in range(2):
-            ts = slice(2 * pair, 2 * pair + 2)
-            nc.scalar.copy(result_c[:, ts, :], banks_c[pair][:])
+        for t in range(PACK):
+            nc.scalar.copy(result_c[:, t : t + 1, :], banks_c[t][:])
         nc.sync.dma_start(out_rows[:, :, cols_c], result_c[:])
-        for ts in (slice(0, 2), slice(2, 4)):
+        for ts in pairs:
             weave(nc.vector.tensor_copy, rounded_c[:, :, ts], result_c[:, ts, :])
         quantize_result(rounded_c, cols_c)
         nc.sync.dma_start(out_words[:, high], out_codes[:, high].bitcast(I32))
 
         out_scale_rows = out_2[0].bitcast(I32)
-        for q in range(4):
+        for q in range(P // QUAD):
             queue = nc.sync if q % 2 else nc.scalar
-            queue.dma_start(out_scale_rows[4 * q : 4 * q + 4, :], out_scale[32 * q : 32 * q + 4, :].bitcast(I32))
+            queue.dma_start(
+                out_scale_rows[PACK * q : PACK * (q + 1), :], out_scale[QUAD * q : QUAD * q + PACK, :].bitcast(I32)
+            )

@@ -14,6 +14,7 @@ U8 = mybir.dt.uint8
 FP8X4 = mybir.dt.float8_e4m3fn_x4
 FP4X4 = mybir.dt.float4_e2m1fn_x4
 GELU = mybir.ActivationFunctionType.Gelu_apprx_tanh
+COPY = mybir.ActivationFunctionType.Copy
 
 P = 128
 PACK = 4
@@ -23,12 +24,13 @@ BLOCK_ROWS = 8
 HALF = S // 2
 CHUNK = 128
 W1_FRONT = 768
-SCALAR_ROUNDS = 64
 BANKS = 8
 
 AT_WORDS = 0
 AT_W2_RAW = 4 * T
 AT_SCALES = AT_W2_RAW + 2 * N
+AT_W1_CODES = AT_SCALES + T
+AT_WOVEN = AT_W1_CODES + 4 * H
 
 
 def tile_picked_permun_gelu_po_kernel(
@@ -82,7 +84,7 @@ def tile_picked_permun_gelu_po_kernel(
         pairs = (slice(0, 2), slice(2, 4))
         for ts in pairs:
             nc.vector.tensor_copy(cast_out[:, :, :, ts], cast_in[:, :, :, ts])
-        w1_codes = keep.tile([P, H], U32, name="w1_codes", align_bytes=64)
+        w1_codes = shared.tile([P, H], U32, name="w1_codes", align_bytes=64, offset=AT_W1_CODES)
         w1_scale = keep.tile([P, H], U8, name="w1_scale", align_bytes=64)
         for ts in pairs:
             dealt = slice(P * ts.start, P * ts.stop)
@@ -110,7 +112,7 @@ def tile_picked_permun_gelu_po_kernel(
             w2s[:].rearrange("p (t m) -> p t m", t=PACK), w2s_raw[:].rearrange("p (m t) -> p t m", t=PACK)
         )
 
-        cols_a, cols_b, cols_c = low, slice(HALF, HALF + CHUNK), slice(HALF + CHUNK, S)
+        cols_b, cols_c = slice(HALF, HALF + CHUNK), slice(HALF + CHUNK, S)
         act = [keep.tile([P, S], F32, name="act%d" % t, align_bytes=64) for t in range(PACK)]
 
         def first_product(bank, t, cols):
@@ -147,94 +149,74 @@ def tile_picked_permun_gelu_po_kernel(
         out_codes = keep.tile([P, S], U32, name="out_codes", align_bytes=64)
         out_scale = keep.tile([P, S], U8, name="out_scale", align_bytes=64)
 
-        def fetch(planes, cols, order):
-            for t in order:
-                nc.vector.tensor_copy(planes[t], act[t][:].indirect(entries(back_sb, cols)))
+        def fetch_on_vector(plane, t, cols):
+            nc.vector.tensor_copy(plane, act[t][:].indirect(entries(back_sb, cols)))
 
-        def weave(engine_copy, woven, planes):
-            engine_copy(woven.rearrange("p (c i) t -> p c t i", i=4), planes.rearrange("p t (c i) -> p c t i", i=4))
+        def fetch_on_scalar(plane, t, cols):
+            nc.scalar.activation(plane, act[t][:].indirect(entries(back_sb, cols)), COPY)
 
-        def quantize_z(z_codes, z_scale, woven):
-            nc.vector.quantize_mx(z_codes[:].bitcast(FP8X4), z_scale[:], woven.rearrange("p n t -> p (n t)"))
-
-        def second_product(z_codes, z_scale, banks):
-            per_bank = PACK // banks
-            width = z_codes.shape[1]
-            tiles = [psum.tile([P, per_bank, width], F32, name="out_bank", tag="bank") for b in range(banks)]
-            for t in range(PACK):
-                nc.tensor.matmul_mx(
-                    tiles[t // per_bank][:, t % per_bank, :],
-                    lhsT=w2w[:, 2 * P * t : 2 * P * (t + 1)].bitcast(FP4X4),
-                    lhsT_scale=w2s[:, P * t : P * (t + 1)],
-                    rhs=z_codes[:].bitcast(FP8X4),
-                    rhs_scale=z_scale[:],
-                    start=True,
-                    stop=True,
-                )
-            return tiles
-
-        def quantize_result(rounded, cols):
-            nc.vector.quantize_mx(
-                out_codes[:, cols].bitcast(FP8X4), out_scale[:, cols], rounded[:].rearrange("p n t -> p (n t)")
+        def weave(woven, planes):
+            nc.vector.tensor_copy(
+                woven.rearrange("p (c i) t -> p c t i", i=4), planes.rearrange("p t (c i) -> p c t i", i=4)
             )
 
-        fetched = shared.tile([P, 9 * CHUNK], BF16, name="fetched", align_bytes=64, offset=AT_W2_RAW)
-        pairs_a = [
-            fetched[:, 4 * CHUNK : 8 * CHUNK].rearrange("p (t n) -> p t n", t=2),
-            fetched[:, : 4 * CHUNK].rearrange("p (t n) -> p t n", t=2),
+        def quantize(codes, scale, woven):
+            nc.vector.quantize_mx(codes.bitcast(FP8X4), scale, woven.rearrange("p n t -> p (n t)"))
+
+        chunks = [slice(CHUNK * c, CHUNK * (c + 1)) for c in range(S // CHUNK)]
+        first, second = slice(0, CHUNK), slice(CHUNK, HALF)
+
+        planes_low = shared.tile([P, PACK, HALF], BF16, name="planes_low", align_bytes=64, offset=AT_W2_RAW)
+        planes_high = shared.tile([P, PACK, HALF], BF16, name="planes_high", align_bytes=64, offset=AT_W1_CODES)
+        for t in range(3):
+            fetch_on_vector(planes_low[:, t, :], t, low)
+        fetch_on_scalar(planes_low[:, 3, first], 3, chunks[0])
+        fetch_on_vector(planes_low[:, 3, second], 3, chunks[1])
+        fetch_on_vector(planes_high[:, 3, :], 3, high)
+        for t in range(3):
+            fetch_on_scalar(planes_high[:, t, :], t, high)
+
+        z_codes = keep.tile([P, S], U32, name="z_codes", align_bytes=64)
+        z_scale = keep.tile([P, S], U8, name="z_scale", align_bytes=64)
+        result = [keep.tile([P, PACK, CHUNK], F32, name="result%d" % c, align_bytes=64) for c in range(4)]
+        rounded = keep.tile([P, S, PACK], BF16, name="rounded", align_bytes=64)
+
+        def second_product(c):
+            cols = chunks[c]
+            for ts in pairs:
+                bank = psum.tile([P, 2, CHUNK], F32, name="out_bank", tag="bank")
+                for t in range(ts.start, ts.stop):
+                    nc.tensor.matmul_mx(
+                        bank[:, t - ts.start, :],
+                        lhsT=w2w[:, 2 * P * t : 2 * P * (t + 1)].bitcast(FP4X4),
+                        lhsT_scale=w2s[:, P * t : P * (t + 1)],
+                        rhs=z_codes[:, cols].bitcast(FP8X4),
+                        rhs_scale=z_scale[:, cols],
+                        start=True,
+                        stop=True,
+                    )
+                nc.scalar.copy(result[c][:, ts, :], bank[:])
+            nc.sync.dma_start(out_rows[:, :, cols], result[c][:])
+
+        woven = [
+            shared.tile([P, CHUNK, PACK], BF16, name="woven%d" % c, align_bytes=64, offset=AT_WOVEN + 1024 * at)
+            for c, at in enumerate((0, 1, 1, 0))
         ]
-        planes_b = fetched[:, 5 * CHUNK :].rearrange("p (t n) -> p t n", t=PACK)
-        planes_c = fetched[:, : 8 * CHUNK].rearrange("p (t n) -> p t n", t=PACK)[:, :, CHUNK:]
-        woven_a = keep.tile([P, HALF, PACK], BF16, name="woven_a", align_bytes=64)
-        woven_b = keep.tile([P, CHUNK, PACK], BF16, name="woven_b", align_bytes=64)
+        for half, planes in enumerate((planes_low, planes_high)):
+            for c, part in ((2 * half, first), (2 * half + 1, second)):
+                weave(woven[c][:], planes[:, :, part])
+            for c in (2 * half, 2 * half + 1):
+                quantize(z_codes[:, chunks[c]], z_scale[:, chunks[c]], woven[c][:])
+                second_product(c)
 
-        fetch([pairs_a[t // 2][:, t % 2, :] for t in range(PACK)], cols_a, range(PACK))
-        for part in (slice(0, CHUNK), slice(CHUNK, HALF)):
-            weave(nc.scalar.copy, woven_a[:, part, pairs[0]], pairs_a[0][:, :, part])
-        weave(nc.scalar.copy, woven_a[:, :, pairs[1]], pairs_a[1])
-        fetch([planes_b[:, t, :] for t in range(PACK)], cols_b, (3, 1, 0, 2))
-        z_codes_a = keep.tile([P, HALF], U32, name="z_codes_a", align_bytes=64)
-        z_scale_a = keep.tile([P, HALF], U8, name="z_scale_a", align_bytes=64)
-        quantize_z(z_codes_a, z_scale_a, woven_a[:])
-        banks_a = second_product(z_codes_a, z_scale_a, PACK)
-        weave(nc.scalar.copy, woven_b[:], planes_b)
-        z_codes_b = keep.tile([P, CHUNK], U32, name="z_codes_b", align_bytes=64)
-        z_scale_b = keep.tile([P, CHUNK], U8, name="z_scale_b", align_bytes=64)
-        quantize_z(z_codes_b, z_scale_b, woven_b[:])
-        banks_b = second_product(z_codes_b, z_scale_b, 1)
-        fetch([planes_c[:, t, :] for t in range(PACK)], cols_c, range(PACK))
-        woven_c = keep.tile([P, CHUNK, PACK], BF16, name="woven_c", align_bytes=64)
-        weave(nc.vector.tensor_copy, woven_c[:], planes_c)
-        z_codes_c = keep.tile([P, CHUNK], U32, name="z_codes_c", align_bytes=64)
-        z_scale_c = keep.tile([P, CHUNK], U8, name="z_scale_c", align_bytes=64)
-        quantize_z(z_codes_c, z_scale_c, woven_c[:])
-        banks_c = second_product(z_codes_c, z_scale_c, PACK)
-
-        result_a = keep.tile([P, PACK, HALF], F32, name="result_a", align_bytes=64)
-        result_b = keep.tile([P, PACK, CHUNK], F32, name="result_b", align_bytes=64)
-        result_c = keep.tile([P, PACK, CHUNK], F32, name="result_c", align_bytes=64)
-        rounded_a = keep.tile([P, HALF, PACK], BF16, name="rounded_a", align_bytes=64)
-        rounded_b = keep.tile([P, CHUNK, PACK], BF16, name="rounded_b", align_bytes=64)
-        rounded_c = keep.tile([P, CHUNK, PACK], BF16, name="rounded_c", align_bytes=64)
-
-        for ts in pairs:
-            for t in range(ts.start, ts.stop):
-                nc.scalar.copy(result_a[:, t : t + 1, :], banks_a[t][:])
-            nc.sync.dma_start(out_rows[:, ts, cols_a], result_a[:, ts, :])
-        nc.scalar.copy(result_b[:], banks_b[0][:])
-        nc.sync.dma_start(out_rows[:, :, cols_b], result_b[:])
-        weave(nc.scalar.copy, rounded_a[:, :SCALAR_ROUNDS, :], result_a[:, :, :SCALAR_ROUNDS])
-        weave(nc.vector.tensor_copy, rounded_a[:, SCALAR_ROUNDS:, :], result_a[:, :, SCALAR_ROUNDS:])
-        weave(nc.vector.tensor_copy, rounded_b[:], result_b[:])
-        quantize_result(rounded_a, cols_a)
-        nc.sync.dma_start(out_words[:, cols_a], out_codes[:, cols_a].bitcast(I32))
-        quantize_result(rounded_b, cols_b)
-        for t in range(PACK):
-            nc.scalar.copy(result_c[:, t : t + 1, :], banks_c[t][:])
-        nc.sync.dma_start(out_rows[:, :, cols_c], result_c[:])
-        for ts in pairs:
-            weave(nc.vector.tensor_copy, rounded_c[:, :, ts], result_c[:, ts, :])
-        quantize_result(rounded_c, cols_c)
+        for c in (0, 1):
+            weave(rounded[:, chunks[c], :], result[c][:])
+        quantize(out_codes[:, low], out_scale[:, low], rounded[:, low, :])
+        nc.sync.dma_start(out_words[:, low], out_codes[:, low].bitcast(I32))
+        for c in (2, 3):
+            weave(rounded[:, chunks[c], :], result[c][:])
+        for c in (2, 3):
+            quantize(out_codes[:, chunks[c]], out_scale[:, chunks[c]], rounded[:, chunks[c], :])
         nc.sync.dma_start(out_words[:, high], out_codes[:, high].bitcast(I32))
 
         out_scale_rows = out_2[0].bitcast(I32)

@@ -178,43 +178,44 @@ def tile_picked_permun_gelu_po_kernel(
 
         z_codes = keep.tile([P, S], U32, name="z_codes", align_bytes=64)
         z_scale = keep.tile([P, S], U8, name="z_scale", align_bytes=64)
-        result = [keep.tile([P, PACK, CHUNK], F32, name="result%d" % c, align_bytes=64) for c in range(4)]
+        result = keep.tile([P, PACK, S], F32, name="result", align_bytes=64)
         rounded = keep.tile([P, S, PACK], BF16, name="rounded", align_bytes=64)
 
-        def second_product(c):
+        def second_product(c, ts):
             cols = chunks[c]
-            for ts in pairs:
-                bank = psum.tile([P, 2, CHUNK], F32, name="out_bank", tag="bank")
-                for t in range(ts.start, ts.stop):
-                    nc.tensor.matmul_mx(
-                        bank[:, t - ts.start, :],
-                        lhsT=w2w[:, 2 * P * t : 2 * P * (t + 1)].bitcast(FP4X4),
-                        lhsT_scale=w2s[:, P * t : P * (t + 1)],
-                        rhs=z_codes[:, cols].bitcast(FP8X4),
-                        rhs_scale=z_scale[:, cols],
-                        start=True,
-                        stop=True,
-                    )
-                nc.scalar.copy(result[c][:, ts, :], bank[:])
-            nc.sync.dma_start(out_rows[:, :, cols], result[c][:])
+            bank = psum.tile([P, 2, CHUNK], F32, name="out_bank", tag="bank")
+            for t in range(ts.start, ts.stop):
+                nc.tensor.matmul_mx(
+                    bank[:, t - ts.start, :],
+                    lhsT=w2w[:, 2 * P * t : 2 * P * (t + 1)].bitcast(FP4X4),
+                    lhsT_scale=w2s[:, P * t : P * (t + 1)],
+                    rhs=z_codes[:, cols].bitcast(FP8X4),
+                    rhs_scale=z_scale[:, cols],
+                    start=True,
+                    stop=True,
+                )
+            nc.scalar.copy(result[:, ts, cols], bank[:])
 
         woven = [
             shared.tile([P, CHUNK, PACK], BF16, name="woven%d" % c, align_bytes=64, offset=AT_WOVEN + 1024 * at)
             for c, at in enumerate((0, 1, 1, 0))
         ]
-        for half, planes in enumerate((planes_low, planes_high)):
+        for half, (planes, cols) in enumerate(((planes_low, low), (planes_high, high))):
             for c, part in ((2 * half, first), (2 * half + 1, second)):
                 weave(woven[c][:], planes[:, :, part])
             for c in (2 * half, 2 * half + 1):
                 quantize(z_codes[:, chunks[c]], z_scale[:, chunks[c]], woven[c][:])
-                second_product(c)
+            for ts in pairs:
+                for c in (2 * half, 2 * half + 1):
+                    second_product(c, ts)
+                nc.sync.dma_start(out_rows[:, ts, cols], result[:, ts, cols])
 
         for c in (0, 1):
-            weave(rounded[:, chunks[c], :], result[c][:])
+            weave(rounded[:, chunks[c], :], result[:, :, chunks[c]])
         quantize(out_codes[:, low], out_scale[:, low], rounded[:, low, :])
         nc.sync.dma_start(out_words[:, low], out_codes[:, low].bitcast(I32))
         for c in (2, 3):
-            weave(rounded[:, chunks[c], :], result[c][:])
+            weave(rounded[:, chunks[c], :], result[:, :, chunks[c]])
         for c in (2, 3):
             quantize(out_codes[:, chunks[c]], out_scale[:, chunks[c]], rounded[:, chunks[c], :])
         nc.sync.dma_start(out_words[:, high], out_codes[:, high].bitcast(I32))

@@ -29,8 +29,6 @@ BANKS = 8
 AT_WORDS = 0
 AT_W2_RAW = 4 * T
 AT_SCALES = AT_W2_RAW + 2 * N
-AT_W1_CODES = AT_SCALES + T
-AT_WOVEN = AT_W1_CODES + 4 * H
 
 
 def tile_picked_permun_gelu_po_kernel(
@@ -84,7 +82,7 @@ def tile_picked_permun_gelu_po_kernel(
         pairs = (slice(0, 2), slice(2, 4))
         for ts in pairs:
             nc.vector.tensor_copy(cast_out[:, :, :, ts], cast_in[:, :, :, ts])
-        w1_codes = shared.tile([P, H], U32, name="w1_codes", align_bytes=64, offset=AT_W1_CODES)
+        w1_codes = keep.tile([P, H], U32, name="w1_codes", align_bytes=64)
         w1_scale = keep.tile([P, H], U8, name="w1_scale", align_bytes=64)
         for ts in pairs:
             dealt = slice(P * ts.start, P * ts.stop)
@@ -164,22 +162,22 @@ def tile_picked_permun_gelu_po_kernel(
             nc.vector.quantize_mx(codes.bitcast(FP8X4), scale, woven.rearrange("p n t -> p (n t)"))
 
         chunks = [slice(CHUNK * c, CHUNK * (c + 1)) for c in range(S // CHUNK)]
-        first, second = slice(0, CHUNK), slice(CHUNK, HALF)
 
-        planes_low = shared.tile([P, PACK, HALF], BF16, name="planes_low", align_bytes=64, offset=AT_W2_RAW)
-        planes_high = shared.tile([P, PACK, HALF], BF16, name="planes_high", align_bytes=64, offset=AT_W1_CODES)
-        for t in range(3):
-            fetch_on_vector(planes_low[:, t, :], t, low)
-        fetch_on_scalar(planes_low[:, 3, first], 3, chunks[0])
-        fetch_on_vector(planes_low[:, 3, second], 3, chunks[1])
-        fetch_on_vector(planes_high[:, 3, :], 3, high)
-        for t in range(3):
-            fetch_on_scalar(planes_high[:, t, :], t, high)
+        strips = shared.tile([P, 32 * CHUNK], BF16, name="strips", align_bytes=64, offset=AT_W2_RAW)
+        planes_low = strips[:, : 12 * CHUNK].rearrange("p (t n) -> p t n", t=PACK)[:, :, :HALF]
+        planes_high = strips[:].rearrange("p (t n) -> p t n", t=PACK)[:, :, :HALF]
+        parts = (slice(0, CHUNK), slice(CHUNK, HALF))
+        planes = [(planes_low, planes_high)[c // 2][:, :, parts[c % 2]] for c in range(4)]
+        woven_all = keep.tile([P, S, PACK], BF16, name="woven_all", align_bytes=64)
+        woven = [woven_all[:, cols, :] for cols in chunks]
 
         z_codes = keep.tile([P, S], U32, name="z_codes", align_bytes=64)
         z_scale = keep.tile([P, S], U8, name="z_scale", align_bytes=64)
         result = keep.tile([P, PACK, S], F32, name="result", align_bytes=64)
         rounded = keep.tile([P, S, PACK], BF16, name="rounded", align_bytes=64)
+
+        def quantize_z(c):
+            quantize(z_codes[:, chunks[c]], z_scale[:, chunks[c]], woven[c])
 
         def second_product(c, ts):
             cols = chunks[c]
@@ -196,28 +194,47 @@ def tile_picked_permun_gelu_po_kernel(
                 )
             nc.scalar.copy(result[:, ts, cols], bank[:])
 
-        woven = [
-            shared.tile([P, CHUNK, PACK], BF16, name="woven%d" % c, align_bytes=64, offset=AT_WOVEN + 1024 * at)
-            for c, at in enumerate((0, 1, 1, 0))
-        ]
-        for half, (planes, cols) in enumerate(((planes_low, low), (planes_high, high))):
-            for c, part in ((2 * half, first), (2 * half + 1, second)):
-                weave(woven[c][:], planes[:, :, part])
-            for c in (2 * half, 2 * half + 1):
-                quantize(z_codes[:, chunks[c]], z_scale[:, chunks[c]], woven[c][:])
+        def second_half(order, cols):
             for ts in pairs:
-                for c in (2 * half, 2 * half + 1):
+                for c in order:
                     second_product(c, ts)
                 nc.sync.dma_start(out_rows[:, ts, cols], result[:, ts, cols])
 
-        for c in (0, 1):
+        def round_result(c):
             weave(rounded[:, chunks[c], :], result[:, :, chunks[c]])
-        quantize(out_codes[:, low], out_scale[:, low], rounded[:, low, :])
+
+        def quantize_result(cols):
+            quantize(out_codes[:, cols], out_scale[:, cols], rounded[:, cols, :])
+
+        for t in range(3):
+            fetch_on_vector(planes_low[:, t, :], t, low)
+        fetch_on_vector(planes_high[:, 2, :], 2, high)
+        for c in (0, 1):
+            fetch_on_scalar(planes[c][:, 3, :], 3, chunks[c])
+        fetch_on_scalar(planes_high[:, 3, :], 3, high)
+        fetch_on_scalar(planes[2][:, 1, :], 1, chunks[2])
+        for c in (0, 1):
+            weave(woven[c], planes[c])
+        quantize_z(0)
+        quantize_z(1)
+        fetch_on_vector(planes[2][:, 0, :], 0, chunks[2])
+        for t in (1, 0):
+            fetch_on_scalar(planes[3][:, t, :], t, chunks[3])
+        second_half((0, 1), low)
+        for c in (2, 3):
+            weave(woven[c], planes[c])
+        for c in (2, 3):
+            quantize_z(c)
+        second_half((2, 3), high)
+
+        for c in (0, 1):
+            round_result(c)
+        quantize_result(low)
         nc.sync.dma_start(out_words[:, low], out_codes[:, low].bitcast(I32))
         for c in (2, 3):
-            weave(rounded[:, chunks[c], :], result[:, :, chunks[c]])
+            round_result(c)
         for c in (2, 3):
-            quantize(out_codes[:, chunks[c]], out_scale[:, chunks[c]], rounded[:, chunks[c], :])
+            quantize_result(chunks[c])
         nc.sync.dma_start(out_words[:, high], out_codes[:, high].bitcast(I32))
 
         out_scale_rows = out_2[0].bitcast(I32)

@@ -95,7 +95,7 @@ def tile_picked_permun_gelu_po_kernel(
         def entries(list_sb, cols):
             return list_sb[:, cols.start // LIST_ROWS : cols.stop // LIST_ROWS]
 
-        low, high, whole = slice(0, HALF), slice(HALF, S), slice(0, S)
+        low, high = slice(0, HALF), slice(HALF, S)
         xw = keep.tile([P, S], U32, name="xw_picked", align_bytes=64)
         for cols in (low, high):
             nc.vector.tensor_copy(xw[:, cols], xw_all[:].bitcast(U32).indirect(entries(offs_sb, cols)))
@@ -110,12 +110,12 @@ def tile_picked_permun_gelu_po_kernel(
             w2s[:].rearrange("p (t m) -> p t m", t=PACK), w2s_raw[:].rearrange("p (m t) -> p t m", t=PACK)
         )
 
-        cols_b, cols_c = slice(HALF, HALF + CHUNK), slice(HALF + CHUNK, S)
         act = [keep.tile([P, S], F32, name="act%d" % t, align_bytes=64) for t in range(PACK)]
 
-        def first_product(bank, t, cols):
+        def first_product(t, cols):
+            bank = psum.tile([P, HALF], F32, name="y_bank", tag="bank")
             nc.tensor.matmul_mx(
-                bank[:, cols],
+                bank[:],
                 lhsT=w1_codes[:, P * t : P * (t + 1)].bitcast(FP8X4),
                 lhsT_scale=w1_scale[:, P * t : P * (t + 1)],
                 rhs=xw[:, cols].bitcast(FP8X4),
@@ -123,24 +123,14 @@ def tile_picked_permun_gelu_po_kernel(
                 start=True,
                 stop=True,
             )
+            nc.scalar.activation(act[t][:, cols], bank[:], GELU)
 
-        def gelu(bank, t, cols):
-            nc.scalar.activation(act[t][:, cols], bank[:, cols], GELU)
-
-        bank_0_low, bank_1, bank_0_third, bank_0_fourth, bank_2, bank_3 = [
-            psum.tile([P, S], F32, name="y_bank", tag="bank") for b in range(PACK + 2)
-        ]
-        first_product(bank_0_low, 0, low)
-        gelu(bank_0_low, 0, low)
-        first_product(bank_1, 1, low)
-        for bank, cols in ((bank_0_third, cols_b), (bank_0_fourth, cols_c)):
-            first_product(bank, 0, cols)
-            gelu(bank, 0, cols)
-        first_product(bank_1, 1, high)
-        gelu(bank_1, 1, whole)
-        for bank, t in ((bank_2, 2), (bank_3, 3)):
-            first_product(bank, t, whole)
-            gelu(bank, t, whole)
+        for cols in (low, high):
+            for t in (0, 1):
+                first_product(t, cols)
+        for t in (2, 3):
+            for cols in (low, high):
+                first_product(t, cols)
 
         out_rows = out_0.rearrange("(p t) j -> p t j", t=PACK)
         out_words = out_1[0].rearrange("p n r -> p (n r)").bitcast(I32)
@@ -168,8 +158,9 @@ def tile_picked_permun_gelu_po_kernel(
         planes_high = strips[:].rearrange("p (t n) -> p t n", t=PACK)[:, :, :HALF]
         parts = (slice(0, CHUNK), slice(CHUNK, HALF))
         planes = [(planes_low, planes_high)[c // 2][:, :, parts[c % 2]] for c in range(4)]
-        woven_all = keep.tile([P, S, PACK], BF16, name="woven_all", align_bytes=64)
-        woven = [woven_all[:, cols, :] for cols in chunks]
+        woven_rest = keep.tile([P, 3, CHUNK, PACK], BF16, name="woven_rest", align_bytes=64)
+        woven = [strips[:, 17 * CHUNK : 21 * CHUNK].rearrange("p (n t) -> p n t", t=PACK)]
+        woven.extend(woven_rest[:, c, :, :] for c in range(3))
 
         z_codes = keep.tile([P, S], U32, name="z_codes", align_bytes=64)
         z_scale = keep.tile([P, S], U8, name="z_scale", align_bytes=64)
@@ -208,7 +199,7 @@ def tile_picked_permun_gelu_po_kernel(
 
         for t in range(3):
             fetch_on_vector(planes_low[:, t, :], t, low)
-        fetch_on_vector(planes_high[:, 2, :], 2, high)
+        fetch_on_vector(planes[2][:, 2, :], 2, chunks[2])
         for c in (0, 1):
             fetch_on_scalar(planes[c][:, 3, :], 3, chunks[c])
         fetch_on_scalar(planes_high[:, 3, :], 3, high)
@@ -218,7 +209,7 @@ def tile_picked_permun_gelu_po_kernel(
         quantize_z(0)
         quantize_z(1)
         fetch_on_vector(planes[2][:, 0, :], 0, chunks[2])
-        for t in (1, 0):
+        for t in (1, 2, 0):
             fetch_on_scalar(planes[3][:, t, :], t, chunks[3])
         second_half((0, 1), low)
         for c in (2, 3):

@@ -153,19 +153,22 @@ def tile_picked_permun_gelu_po_kernel(
 
         chunks = [slice(CHUNK * c, CHUNK * (c + 1)) for c in range(S // CHUNK)]
 
-        strips = shared.tile([P, 32 * CHUNK], BF16, name="strips", align_bytes=64, offset=AT_W2_RAW)
+        strips = shared.tile([P, 33 * CHUNK], BF16, name="strips", align_bytes=64, offset=AT_W2_RAW)
         planes_low = strips[:, : 12 * CHUNK].rearrange("p (t n) -> p t n", t=PACK)[:, :, :HALF]
-        planes_high = strips[:].rearrange("p (t n) -> p t n", t=PACK)[:, :, :HALF]
+        planes_high = strips[:, : 32 * CHUNK].rearrange("p (t n) -> p t n", t=PACK)[:, :, :HALF]
         parts = (slice(0, CHUNK), slice(CHUNK, HALF))
         planes = [(planes_low, planes_high)[c // 2][:, :, parts[c % 2]] for c in range(4)]
-        woven_rest = keep.tile([P, 3, CHUNK, PACK], BF16, name="woven_rest", align_bytes=64)
-        woven = [strips[:, 17 * CHUNK : 21 * CHUNK].rearrange("p (n t) -> p n t", t=PACK)]
-        woven.extend(woven_rest[:, c, :, :] for c in range(3))
+        woven_own = keep.tile([P, HALF, PACK], BF16, name="woven_own", align_bytes=64)
+        woven_0, woven_3 = [
+            strips[:, at * CHUNK : (at + PACK) * CHUNK].rearrange("p (n t) -> p n t", t=PACK) for at in (17, 21)
+        ]
+        woven = [woven_0, woven_own[:, parts[0], :], woven_own[:, parts[1], :], woven_3]
 
         z_codes = keep.tile([P, S], U32, name="z_codes", align_bytes=64)
         z_scale = keep.tile([P, S], U8, name="z_scale", align_bytes=64)
         result = keep.tile([P, PACK, S], F32, name="result", align_bytes=64)
-        rounded = keep.tile([P, S, PACK], BF16, name="rounded", align_bytes=64)
+        rounded_high = keep.tile([P, HALF, PACK], BF16, name="rounded_high", align_bytes=64)
+        rounded = [strips[:, 25 * CHUNK :].rearrange("p (n t) -> p n t", t=PACK), rounded_high[:]]
 
         def quantize_z(c):
             quantize(z_codes[:, chunks[c]], z_scale[:, chunks[c]], woven[c])
@@ -185,17 +188,16 @@ def tile_picked_permun_gelu_po_kernel(
                 )
             nc.scalar.copy(result[:, ts, cols], bank[:])
 
-        def second_half(order, cols):
+        def product_and_store(c):
             for ts in pairs:
-                for c in order:
-                    second_product(c, ts)
-                nc.sync.dma_start(out_rows[:, ts, cols], result[:, ts, cols])
+                second_product(c, ts)
+            nc.sync.dma_start(out_rows[:, :, chunks[c]], result[:, :, chunks[c]])
 
         def round_result(c):
-            weave(rounded[:, chunks[c], :], result[:, :, chunks[c]])
+            weave(rounded[c // 2][:, parts[c % 2], :], result[:, :, chunks[c]])
 
-        def quantize_result(cols):
-            quantize(out_codes[:, cols], out_scale[:, cols], rounded[:, cols, :])
+        def quantize_result(cols, rounded_part):
+            quantize(out_codes[:, cols], out_scale[:, cols], rounded_part)
 
         for t in range(3):
             fetch_on_vector(planes_low[:, t, :], t, low)
@@ -211,21 +213,23 @@ def tile_picked_permun_gelu_po_kernel(
         fetch_on_vector(planes[2][:, 0, :], 0, chunks[2])
         for t in (1, 2, 0):
             fetch_on_scalar(planes[3][:, t, :], t, chunks[3])
-        second_half((0, 1), low)
+        for c in (0, 1):
+            product_and_store(c)
         for c in (2, 3):
             weave(woven[c], planes[c])
-        for c in (2, 3):
             quantize_z(c)
-        second_half((2, 3), high)
+        for c in (2, 3):
+            product_and_store(c)
 
         for c in (0, 1):
             round_result(c)
-        quantize_result(low)
+        for c in (0, 1):
+            quantize_result(chunks[c], rounded[0][:, parts[c], :])
         nc.sync.dma_start(out_words[:, low], out_codes[:, low].bitcast(I32))
         for c in (2, 3):
             round_result(c)
         for c in (2, 3):
-            quantize_result(chunks[c])
+            quantize_result(chunks[c], rounded[1][:, parts[c % 2], :])
         nc.sync.dma_start(out_words[:, high], out_codes[:, high].bitcast(I32))
 
         out_scale_rows = out_2[0].bitcast(I32)

from contextlib import ExitStack

import concourse.mybir as mybir

K, T, S, H, N = 512, 2048, 512, 512, 512
FLOPS = 2 * K * H * S + 2 * H * N * S

F32 = mybir.dt.float32
BF16 = mybir.dt.bfloat16
I32 = mybir.dt.int32
U32 = mybir.dt.uint32
U16 = mybir.dt.uint16
U8 = mybir.dt.uint8
FP8X4 = mybir.dt.float8_e4m3fn_x4
FP4X4 = mybir.dt.float4_e2m1fn_x4
GELU = mybir.ActivationFunctionType.Gelu_apprx_tanh
COPY = mybir.ActivationFunctionType.Copy

P = 128
PACK = 4
LIST_ROWS = 16
QUAD = 32
BLOCK_ROWS = 8
HALF = S // 2
CHUNK = 128
W1_FRONT = 768
BANKS = 8

AT_WORDS = 0
AT_W2_RAW = 4 * T
AT_SCALES = AT_W2_RAW + 2 * N


def tile_picked_permun_gelu_po_kernel(
    tc, x_words, x_scales, w1, w2_words, w2_scales, offs, back, out_0, out_1, out_2
):
    nc = tc.nc
    with ExitStack() as ctx:
        keep = ctx.enter_context(tc.tile_pool(name="keep", bufs=1))
        shared = ctx.enter_context(tc.tile_pool(name="shared", bufs=1))
        psum = ctx.enter_context(tc.psum_pool(name="psum", bufs=BANKS))

        offs_sb = keep.tile([P, S // LIST_ROWS], U16, name="offs_sb")
        back_sb = keep.tile([P, S // LIST_ROWS], U16, name="back_sb")
        xs_mm = keep.tile([P, S], U8, name="xs_mm", align_bytes=64)
        w1_raw = keep.tile([P, PACK, H], F32, name="w1_raw", align_bytes=64)
        xw_all = shared.tile([P, T], I32, name="xw_all", align_bytes=64, offset=AT_WORDS)
        w2w_raw = shared.tile([P, 2 * N], U8, name="w2w_raw", align_bytes=64, offset=AT_W2_RAW)
        xs_all = shared.tile([P, T], U8, name="xs_all", align_bytes=64, offset=AT_SCALES)

        nc.vector.memset(xs_all[:].bitcast(I32), 0)

        w1_rows = w1.rearrange("(p j) c -> p (j c)", j=PACK)
        w1_flat = w1_raw[:].rearrange("p j c -> p (j c)")
        nc.sync.dma_start(w1_flat[:, :W1_FRONT], w1_rows[:, :W1_FRONT])
        nc.sync.dma_start(offs_sb[:], offs)
        nc.sync.dma_start(back_sb[:], back)
        nc.sync.dma_start(xs_all[0:P:BLOCK_ROWS, :].bitcast(I32), x_scales[0].bitcast(I32))
        nc.sync.dma_start(w1_flat[:, W1_FRONT:], w1_rows[:, W1_FRONT:])
        nc.sync.dma_start(xw_all[:], x_words[0].rearrange("p n r -> p (n r)").bitcast(I32))
        nc.sync.dma_start(w2w_raw[:].bitcast(I32), w2_words[0].bitcast(I32))

        xs_picked = keep.tile([P, S], U8, name="xs_picked", align_bytes=64)
        nc.vector.tensor_copy(xs_picked[:], xs_all[:].indirect(offs_sb[:]))
        nc.vector.tensor_copy(xs_mm[:].bitcast(I32), xs_picked[:].bitcast(I32))
        for r in range(1, PACK):
            nc.scalar.dma_start(
                xs_mm[r:P:QUAD, :].bitcast(I32), xs_picked[BLOCK_ROWS * r : P : QUAD, :].bitcast(I32)
            )

        w2s_raw = shared.tile([P, N], U8, name="w2s_raw", align_bytes=64, offset=AT_SCALES)
        nc.gpsimd.memset(w2s_raw[:].bitcast(I32), 0)
        for q in range(P // QUAD):
            nc.sync.dma_start(
                w2s_raw[QUAD * q : QUAD * q + PACK, :].bitcast(I32),
                w2_scales[0, PACK * q : PACK * (q + 1), :].bitcast(I32),
            )

        w1_bf = keep.tile([P, PACK * H], BF16, name="w1_bf", align_bytes=64)
        cast_out = w1_bf[:].rearrange("p (t m j) -> p m j t", t=PACK, j=PACK)
        cast_in = w1_raw[:].rearrange("p j (m t) -> p m j t", t=PACK)
        pairs = (slice(0, 2), slice(2, 4))
        for ts in pairs:
            nc.vector.tensor_copy(cast_out[:, :, :, ts], cast_in[:, :, :, ts])
        w1_codes = keep.tile([P, H], U32, name="w1_codes", align_bytes=64)
        w1_scale = keep.tile([P, H], U8, name="w1_scale", align_bytes=64)
        for ts in pairs:
            dealt = slice(P * ts.start, P * ts.stop)
            nc.vector.quantize_mx(
                w1_codes[:, dealt].bitcast(FP8X4),
                w1_scale[:, dealt],
                w1_bf[:, PACK * dealt.start : PACK * dealt.stop],
            )

        def entries(list_sb, cols):
            return list_sb[:, cols.start // LIST_ROWS : cols.stop // LIST_ROWS]

        low, high = slice(0, HALF), slice(HALF, S)
        xw = keep.tile([P, S], U32, name="xw_picked", align_bytes=64)
        for cols in (low, high):
            nc.vector.tensor_copy(xw[:, cols], xw_all[:].bitcast(U32).indirect(entries(offs_sb, cols)))

        w2w = shared.tile([P, 2 * N], U8, name="w2w", align_bytes=64, offset=AT_WORDS)
        nc.vector.tensor_copy(
            w2w[:].bitcast(U16).rearrange("p (t m) -> p t m", t=PACK),
            w2w_raw[:].bitcast(U16).rearrange("p (m t) -> p t m", t=PACK),
        )
        w2s = shared.tile([P, N], U8, name="w2s", align_bytes=64, offset=AT_WORDS + 2 * N)
        nc.vector.tensor_copy(
            w2s[:].rearrange("p (t m) -> p t m", t=PACK), w2s_raw[:].rearrange("p (m t) -> p t m", t=PACK)
        )

        act = [keep.tile([P, S], F32, name="act%d" % t, align_bytes=64) for t in range(PACK)]

        def first_product(t, cols):
            bank = psum.tile([P, HALF], F32, name="y_bank", tag="bank")
            nc.tensor.matmul_mx(
                bank[:],
                lhsT=w1_codes[:, P * t : P * (t + 1)].bitcast(FP8X4),
                lhsT_scale=w1_scale[:, P * t : P * (t + 1)],
                rhs=xw[:, cols].bitcast(FP8X4),
                rhs_scale=xs_mm[:, cols],
                start=True,
                stop=True,
            )
            nc.scalar.activation(act[t][:, cols], bank[:], GELU)

        for cols in (low, high):
            for t in (0, 1):
                first_product(t, cols)
        for t in (2, 3):
            for cols in (low, high):
                first_product(t, cols)

        out_rows = out_0.rearrange("(p t) j -> p t j", t=PACK)
        out_words = out_1[0].rearrange("p n r -> p (n r)").bitcast(I32)
        out_codes = keep.tile([P, S], U32, name="out_codes", align_bytes=64)
        out_scale = keep.tile([P, S], U8, name="out_scale", align_bytes=64)

        def fetch_on_vector(plane, t, cols):
            nc.vector.tensor_copy(plane, act[t][:].indirect(entries(back_sb, cols)))

        def fetch_on_scalar(plane, t, cols):
            nc.scalar.activation(plane, act[t][:].indirect(entries(back_sb, cols)), COPY)

        def weave(woven, planes):
            nc.vector.tensor_copy(
                woven.rearrange("p (c i) t -> p c t i", i=4), planes.rearrange("p t (c i) -> p c t i", i=4)
            )

        def quantize(codes, scale, woven):
            nc.vector.quantize_mx(codes.bitcast(FP8X4), scale, woven.rearrange("p n t -> p (n t)"))

        chunks = [slice(CHUNK * c, CHUNK * (c + 1)) for c in range(S // CHUNK)]

        strips = shared.tile([P, 33 * CHUNK], BF16, name="strips", align_bytes=64, offset=AT_W2_RAW)
        planes_low = strips[:, : 12 * CHUNK].rearrange("p (t n) -> p t n", t=PACK)[:, :, :HALF]
        planes_high = strips[:, : 32 * CHUNK].rearrange("p (t n) -> p t n", t=PACK)[:, :, :HALF]
        parts = (slice(0, CHUNK), slice(CHUNK, HALF))
        planes = [(planes_low, planes_high)[c // 2][:, :, parts[c % 2]] for c in range(4)]
        woven_own = keep.tile([P, HALF, PACK], BF16, name="woven_own", align_bytes=64)
        woven_0, woven_3 = [
            strips[:, at * CHUNK : (at + PACK) * CHUNK].rearrange("p (n t) -> p n t", t=PACK) for at in (17, 21)
        ]
        woven = [woven_0, woven_own[:, parts[0], :], woven_own[:, parts[1], :], woven_3]

        z_codes = keep.tile([P, S], U32, name="z_codes", align_bytes=64)
        z_scale = keep.tile([P, S], U8, name="z_scale", align_bytes=64)
        result = keep.tile([P, PACK, S], F32, name="result", align_bytes=64)
        rounded_high = keep.tile([P, HALF, PACK], BF16, name="rounded_high", align_bytes=64)
        rounded = [strips[:, 25 * CHUNK :].rearrange("p (n t) -> p n t", t=PACK), rounded_high[:]]

        def quantize_z(c):
            quantize(z_codes[:, chunks[c]], z_scale[:, chunks[c]], woven[c])

        def second_product(c, ts):
            cols = chunks[c]
            bank = psum.tile([P, 2, CHUNK], F32, name="out_bank", tag="bank")
            for t in range(ts.start, ts.stop):
                nc.tensor.matmul_mx(
                    bank[:, t - ts.start, :],
                    lhsT=w2w[:, 2 * P * t : 2 * P * (t + 1)].bitcast(FP4X4),
                    lhsT_scale=w2s[:, P * t : P * (t + 1)],
                    rhs=z_codes[:, cols].bitcast(FP8X4),
                    rhs_scale=z_scale[:, cols],
                    start=True,
                    stop=True,
                )
            nc.scalar.copy(result[:, ts, cols], bank[:])

        def product_and_store(c):
            for ts in pairs:
                second_product(c, ts)
            nc.sync.dma_start(out_rows[:, :, chunks[c]], result[:, :, chunks[c]])

        def round_result(c):
            weave(rounded[c // 2][:, parts[c % 2], :], result[:, :, chunks[c]])

        def quantize_result(cols, rounded_part):
            quantize(out_codes[:, cols], out_scale[:, cols], rounded_part)

        for t in range(3):
            fetch_on_vector(planes_low[:, t, :], t, low)
        fetch_on_vector(planes[2][:, 2, :], 2, chunks[2])
        for c in (0, 1):
            fetch_on_scalar(planes[c][:, 3, :], 3, chunks[c])
        fetch_on_scalar(planes_high[:, 3, :], 3, high)
        fetch_on_scalar(planes[2][:, 1, :], 1, chunks[2])
        for c in (0, 1):
            weave(woven[c], planes[c])
        quantize_z(0)
        quantize_z(1)
        fetch_on_vector(planes[2][:, 0, :], 0, chunks[2])
        for t in (1, 2, 0):
            fetch_on_scalar(planes[3][:, t, :], t, chunks[3])
        for c in (0, 1):
            product_and_store(c)
        for c in (2, 3):
            weave(woven[c], planes[c])
            quantize_z(c)
        for c in (2, 3):
            product_and_store(c)

        for c in (0, 1):
            round_result(c)
        for c in (0, 1):
            quantize_result(chunks[c], rounded[0][:, parts[c], :])
        nc.sync.dma_start(out_words[:, low], out_codes[:, low].bitcast(I32))
        for c in (2, 3):
            round_result(c)
        for c in (2, 3):
            quantize_result(chunks[c], rounded[1][:, parts[c % 2], :])
        nc.sync.dma_start(out_words[:, high], out_codes[:, high].bitcast(I32))

        out_scale_rows = out_2[0].bitcast(I32)
        for q in range(P // QUAD):
            queue = nc.sync if q % 2 else nc.scalar
            queue.dma_start(
                out_scale_rows[PACK * q : PACK * (q + 1), :], out_scale[QUAD * q : QUAD * q + PACK, :].bitcast(I32)
            )
